import numpy as np, ml_dtypes
CORES = [36,164,52,180,100,228,116,244]
N = 8
BF = ml_dtypes.bfloat16
def gentries(a):
    return np.ascontiguousarray(a.reshape(8, 16, -1).transpose(0, 2, 1)).reshape(8, -1)
def gtable(e):
    e = np.asarray(e); return np.ascontiguousarray(e.reshape(8, -1, 16).transpose(0, 2, 1)).reshape(128, -1).astype(np.int32)
W, L, RO, PE, ES, LAST = 4096, 192, 3, 3, 4, 1
def names(rng): return rng.integers(0, W, (N, 8, L, 16))
def pack(x, s, z):
    return {"cont": np.ascontiguousarray(np.reshape(x, (N, 128, W))).astype(np.float32).astype(BF),
            "enz": np.stack([gtable(a.reshape(8, -1)) for a in s]), "subs": np.stack([gtable(a.reshape(8, -1)) for a in z])}
def setup_inputs(rng):
    x = np.where(rng.random((N, 8, 1, W)) < 0.3, 51 * rng.integers(0, 6, (N, 8, 16, W)), rng.integers(0, 256, (N, 8, 16, W)))
    s, z = names(rng), names(rng); u = rng.random((N, 8, L, 1))
    z = np.where((u < 0.15) & (rng.random(z.shape) < 0.3), s[..., 15:], z)
    z = np.where((u > 0.9) & (rng.random(z.shape) < 0.5), z[..., 7:8], z)
    return pack(x, s, z)
def setup_inputs_spread(rng):
    x = np.minimum((np.exp2(3 + 5.5 * rng.random((N, 8, 1, W))) * rng.random((N, 8, 16, W))).astype(np.int64), 255)
    e = rng.choice(np.array([1.0, 1.5, 2.0, 3.0, 4.0]), (N, 8, 1, 1))
    s = np.minimum((W * rng.random((N, 8, L, 16)) ** e).astype(np.int64), W - 1)
    z = W - 1 - np.minimum((W * rng.random((N, 8, L, 16)) ** e).astype(np.int64), W - 1)
    return pack(x, s, z)
def setup_inputs_ends(rng):
    x = 255 * (rng.random((N, 8, 16, W)) < rng.choice(np.array([0.0, 0.1, 0.3, 0.5, 0.7, 0.9, 1.0]), (N, 8, 1, W)))
    near = (np.arange(16)[:, None] == rng.integers(0, 16, (N, 8, 1, W))) & (rng.random((N, 8, 1, W)) < 0.3)
    x = np.where(near, np.where(x == 0, 1, 254), x)
    m = np.stack([np.concatenate([rng.permutation(np.array([0, 10, 6, 8, 7, 9, 12])), np.array([16])]) for q in range(N)])
    top = np.argsort(rng.random((N, 8, 16)), axis=-1) < m[..., None]
    x[..., W - 1] = np.where(top, 255, 0); x[..., 0] = np.where(top, 0, 255)
    x[:, 7, :, W - 2] = 255; x[:, 7, 15, W - 2] = 254; x[:, 7, :, 1] = 0; x[:, 7, 0, 1] = 1
    x[:, 7, :, W - 3] = 255; x[:, 7, 14:, W - 3] = 254
    sz = []
    for i in range(2):
        fr = rng.choice(np.array([1.0, 0.6]), (N, 8, L, 1))
        sz.append(np.where(rng.random((N, 8, L, 16)) < fr, (W - 1) * rng.integers(0, 2, (N, 8, L, 16)), names(rng)))
    s, z = sz; alt = np.where(np.arange(16) & 1 == 1, W - 1, 0)
    for a, b, c in ((L - 1, L - 2, L - 3), (0, 1, 2)):
        s[:, 7, a] = W - 1 - alt; z[:, 7, a] = W - 1; z[:, 7, a, 9] = W - 2; z[:, 7, a, 15] = W - 2
        s[:, 7, b] = alt; z[:, 7, b] = 0
        s[:, 7, c] = alt; z[:, 7, c] = W - 1
        z[:, 7, c, 5] = W - 31
    for i, (p1, p2) in enumerate(((6, 11), (1, 14), (0, 15))):
        for a in (L - 4 - i, 3 + i):
            s[:, 7, a] = W - 1 - alt; z[:, 7, a] = W - 1; z[:, 7, a, p1] = W - 2; z[:, 7, a, p2] = W - 3
    return pack(x, s, z)
def setup_inputs_corners(rng):
    B = W // 16; kind = rng.integers(0, 7, (N, 8, B))
    for q in range(N):
        g = rng.permutation(8); kind[q, g[0]] = 0; kind[q, g[1]] = 3
    opts = ([0, 2, 4], [0, 2, 4], [5, 7, 9, 11], [6, 7, 8, 9], [10, 11, 12, 13], [5, 6, 7, 9, 10], list(range(17)))
    cs = np.zeros((N, 8, B, 16), np.int64)
    for i, o in enumerate(opts): cs = np.where(kind[..., None] == i, rng.choice(np.array(o), cs.shape), cs)
    cs[..., 0] = np.where(kind == 1, rng.choice(np.array([1, 3, 5]), kind.shape), cs[..., 0])
    down = (np.argsort(rng.random((N, 8, B, 16, 16)), axis=-1) < cs[..., None]).transpose(0, 1, 2, 4, 3).copy()
    down[..., 0] &= ~np.all(down, axis=-1)
    st = rng.integers(1, 17, down.shape); v = np.zeros(down.shape, np.int64); cur = np.full(down.shape[:-1], 255)
    for k in range(32):
        v[..., k & 15] = cur; cur = np.where(down[..., k & 15], cur - st[..., k & 15], 255)
    x = np.ascontiguousarray(v.transpose(0, 1, 3, 2, 4)).reshape(N, 8, 16, W)
    blk = np.concatenate([np.argsort(rng.random((N, 8, B)), axis=-1) for i in range(2)], axis=-1)[..., :L]
    rot = np.where(np.arange(L) < B, 0, rng.integers(0, 16, (N, 8, L)))
    s = 16 * blk[..., None] + ((np.arange(16) + rot[..., None]) & 15)
    inv = np.argsort(rng.random((N, 8, W)), axis=-1); new = np.argsort(inv, axis=-1)
    x = np.take_along_axis(x, inv[:, :, None], 3); s = np.take_along_axis(new, s.reshape(N, 8, -1), 2).reshape(N, 8, L, 16)
    one = rng.choice(np.array([0, W - 1, W // 2, 5]), (N, 8, L, 1)); s = np.where(rng.random((N, 8, L, 1)) < 0.1, one, s)
    z = names(rng); zk = rng.integers(0, 7, (N, 8, L, 1)); p = np.arange(16); own = s[..., 15:]
    z = np.where((zk == 1) & (p == 15), own, z); z = np.where((zk == 2) & ((p == 0) | (p == 15)), own, z)
    z = np.where(zk == 3, own, z); z = np.where(zk == 4, s, z)
    z = np.where(zk == 5, (W - 1) * rng.integers(0, 2, z.shape), z); z = np.where((zk == 6) & (p == rng.integers(0, 16, zk.shape)), own, z)
    return pack(x, s, z)
def setup_inputs_ties(rng):
    lev = np.array([[0, 1, 254, 255], [3, 4, 5, 250]])[np.arange(8) & 1]
    x = np.take_along_axis(np.broadcast_to(lev[None], (N, 8, 4)), rng.integers(0, 4, (N, 8, 16 * W)), 2).reshape(N, 8, 16, W)
    pool = rng.integers(0, W, (N, 8, 24)); pool[..., 0] = 0; pool[..., 1] = W - 1
    s = np.take_along_axis(pool, rng.integers(0, 24, (N, 8, L * 16)), 2).reshape(N, 8, L, 16)
    z = np.take_along_axis(pool, rng.integers(0, 24, (N, 8, L * 16)), 2).reshape(N, 8, L, 16)
    u = rng.random((N, 8, L, 1)); z = np.where(u < 0.2, s, z); z = np.where(u > 0.85, z[..., 3:4], z)
    return pack(x, s, z)
def setup_inputs_full(rng):
    B = W // 16; kind = np.stack([rng.permutation(np.array([0, 0, 0, 1, 1, 2, 2, 2])) for q in range(N)]); kind[0, 7] = 1; kind[N - 1, 7] = 0
    k4 = kind[:, :, None, None]
    cs = np.where(k4 == 0, rng.choice(np.array([10, 12, 14]), (N, 8, B, 16)), rng.integers(6, 16, (N, 8, B, 16)))
    cs[..., 0] += ((kind[:, :, None] == 0) & (rng.random((N, 8, B)) < 0.5)).astype(np.int64)
    t1 = np.argsort(rng.random((N, 8, B, 16)), axis=-1); t2 = np.argsort(rng.random((N, 8, B, 16)), axis=-1)
    down = ((t1[..., :, None] + t2[..., None, :]) & 15) < cs[..., None, :]
    st = rng.integers(1, 17, down.shape); v = np.zeros(down.shape, np.int64); cur = np.full(down.shape[:-1], 255)
    for k in range(32):
        v[..., k & 15] = cur; cur = np.where(down[..., k & 15], cur - st[..., k & 15], 255)
    x = np.ascontiguousarray(v.transpose(0, 1, 3, 2, 4)).reshape(N, 8, 16, W)
    blk = np.concatenate([np.argsort(rng.random((N, 8, B)), axis=-1) for i in range(2)], axis=-1)[..., :L]
    s = 16 * blk[..., None] + np.arange(16)
    inv = np.argsort(rng.random((N, 8, W)), axis=-1); new = np.argsort(inv, axis=-1)
    x = np.take_along_axis(x, inv[:, :, None], 3); s = np.take_along_axis(new, s.reshape(N, 8, -1), 2).reshape(N, 8, L, 16)
    hi = np.arange(W - 96, W); ok = ((hi[:, None] * np.arange(W) >> 5) & (W - 1)) + hi[:, None] + 77 == 2 * W
    made = np.where(np.any(ok, axis=1), np.argmax(ok, axis=1), -1); y = W - 32 + ((-((hi & 31) ** 7)) & 31)
    mate = np.full(W, -1); mate[W - 96:] = np.where(((hi & 1) == 1) & (hi * (y + 32) > 2 ** 24), y, made)
    zu = np.where(mate[s] >= 0, mate[s], names(rng)); zu[..., 0] = s[..., 15]
    way = 1 - 2 * (np.take_along_axis(cs[..., 0], blk, 2) & 1)
    p = (rng.integers(0, 16, (N, 8, L, 1)) + way[..., None] * np.arange(16)) & 15
    z = np.take_along_axis(zu, np.argsort(p, axis=-1), 3)
    z = np.where(rng.random((N, 8, L, 1)) < 0.75, z, names(rng))
    pm = np.argsort(rng.random((N, 8, W)), axis=-1); cl = (np.argsort(pm, axis=-1) >> 9)[:, :, None]
    few = rng.integers(0, 4, (N, 8, 16, W)); x2 = rng.integers(0, 256, (N, 8, 16, W)); x2 = np.where(cl == 0, few, x2)
    for i, b in ((1, 134), (2, 198), (3, 255)): x2 = np.where(cl == i, b - few, x2)
    s2 = names(rng); s2[..., 15] = np.take_along_axis(pm, rng.integers(0, 512, (N, 8, L)), 2)
    zi = 512 * rng.integers(1, 4, (N, 8, L, 1)) + rng.integers(0, 512, (N, 8, L, 16))
    z2 = np.take_along_axis(pm, zi.reshape(N, 8, -1), 2).reshape(N, 8, L, 16)
    return pack(np.where(k4 == 2, x2, x), np.where(k4 == 2, s2, s), np.where(k4 == 2, z2, z))
def check_inputs(d):
    bad = []
    c = np.asarray(d["cont"]).astype(np.float32)
    if not np.all((c >= 0) & (c <= 255)): bad.append("range of cont")
    elif not np.all(c == np.floor(c)): bad.append("whole numbers in cont")
    for k in ("enz", "subs"):
        if np.min(d[k]) < 0 or np.max(d[k]) > W - 1: bad.append("range of " + k)
    return bad
def edit(x, s, z, a, t):
    v = np.take_along_axis(x, s.reshape(8, 1, -1), 2).reshape(8, 16, L, 16)
    y = np.take_along_axis(x, z.reshape(8, 1, -1), 2).reshape(8, 16, L, 16)
    c = np.sum((v > np.roll(v, -1, axis=3)).astype(np.int64), axis=1)
    dist = np.sum(np.abs(y - v[..., 15:16]).astype(np.int64), axis=1)
    step = 1 - 2 * (np.add.accumulate(c, axis=2) & 1); step[..., 0] = np.argmin(dist, axis=2)
    pos = np.add.accumulate(step, axis=2) & 15
    hit = pos[:, :, None, :] == np.arange(16)[:, None]
    e = 15 - np.argmax(hit[..., ::-1], axis=3) if LAST else np.argmax(hit, axis=3)
    has = np.any(hit, axis=3); ce = np.take_along_axis(c, e, 2); se = np.take_along_axis(s, e, 2)
    gone = has & (ce <= 5 + (a & 1)[..., None])
    new = np.where(has, np.where(ce <= 9, se, ((se * z >> 5) + se + 77 * t) & (W - 1)), z)
    n = np.sum(gone.astype(np.int64), axis=2); i = np.arange(16) - (16 - n)[..., None]
    kept = np.take_along_axis(new, np.argsort(gone, axis=2, kind="stable"), 2)
    return np.where(i < 0, kept, np.take_along_axis(s, np.maximum(i, 0), 2)), n
def reference(cont, enz, subs):
    x = cont.astype(np.float32).astype(np.int16).reshape(N, 8, 16, W)
    s = np.stack([gentries(a) for a in enz]).astype(np.int64).reshape(N, 8, L, 16)
    z = np.stack([gentries(a) for a in subs]).astype(np.int64).reshape(N, 8, L, 16)
    dels = np.zeros((N, 8, L), np.int64)
    for t in range(1, RO + 1):
        both = [edit(x[r], s[r], z[r], dels[r], t) for r in range(N)]
        dels = np.stack([b[1] for b in both])
        z = np.roll(s, ES, axis=0)
        s = np.roll(np.stack([b[0] for b in both]), PE, axis=0)
    return {"yenz": np.stack([gtable(a.reshape(8, -1)) for a in s]).astype(np.float32), "ysub": np.stack([gtable(a.reshape(8, -1)) for a in z]).astype(np.float32)}

@@ -1,0 +1,443 @@
+from concourse.bass import DstId, RemoteDMATransfer
+from concourse.mybir import dt, AluOpType as A, ActivationFunctionType as F
+
+H = 3
+NL = 4
+R = 3
+CY = 0.83
+PCY = 0.42
+BIG = 1.0e9
+LATE, HOLD, AHEAD, PASSES = 100, 400.0, 0.8, 4
+ON_VECTOR = ((1, 0, "v"),)
+
+SCRATCH = {
+    "ct": ("sbuf", [128, 4096], "bfloat16"),
+    "en": ("sbuf", [128, 192], "int32"), "su": ("sbuf", [128, 192], "int32"),
+    "one": ("sbuf", [128, 128], "float32"), "idf": ("sbuf", [128, 128], "float32"),
+    "g8a": ("sbuf", [128, 8], "float32"), "g8b": ("sbuf", [128, 8], "float32"), "g8c": ("sbuf", [128, 8], "float32"),
+    "pid": ("sbuf", [128, 1], "int32"), "pbit": ("sbuf", [128, 1], "int32"),
+    "modd": ("sbuf", [128, 1], "float32"), "meven": ("sbuf", [128, 1], "float32"),
+    "selc": ("sbuf", [128, 160], "bfloat16"), "seld": ("sbuf", [128, 160], "bfloat16"),
+    "ip": ("sbuf", [128, 128], "bfloat16"), "im": ("sbuf", [128, 128], "bfloat16"),
+    "i16th": ("sbuf", [128, 128], "bfloat16"), "i8192": ("sbuf", [128, 128], "bfloat16"),
+    "i2048": ("sbuf", [128, 128], "bfloat16"), "i16": ("sbuf", [128, 128], "bfloat16"), "i32": ("sbuf", [128, 128], "bfloat16"),
+    "im256": ("sbuf", [128, 128], "bfloat16"), "iph": ("sbuf", [128, 128], "float16"),
+    "kc8": ("sbuf", [128, 64], "bfloat16"), "krow": ("sbuf", [128, 64], "bfloat16"),
+    "kw": ("sbuf", [128, 68], "bfloat16"),
+    "kkeep": ("sbuf", [128, 64], "bfloat16"), "kfill": ("sbuf", [128, 64], "bfloat16"),
+    "mk17": ("sbuf", [128, 68], "float32"), "rk17": ("sbuf", [128, 68], "float32"),
+    "rm17": ("sbuf", [128, 68], "float32"), "rn17": ("sbuf", [128, 68], "float32"),
+    "mk16": ("sbuf", [128, 64], "float32"), "rm16": ("sbuf", [128, 64], "float32"),
+    "m0": ("sbuf", [128, H, 128], "uint16"), "ls2": ("sbuf", [128, H, 128], "uint16"),
+    "pdiff0": ("psum", [128, 512], "float32"), "pdiff1": ("psum", [128, 512], "float32"),
+    "pck": ("psum", [128, 4, 2, 16, NL], "float32"),
+    "pu0": ("psum", [128, 2, NL, 64], "float32"), "pu1": ("psum", [128, 2, NL, 64], "float32"),
+    "pe0": ("psum", [128, 8, NL, 16], "float32"), "pe1": ("psum", [128, 8, NL, 16], "float32"),
+    "pw": ("psum", [128, 8, 64], "float32"),
+}
+for _k in ("e", "s"):
+    SCRATCH["xm" + _k] = ("sbuf", [128, 12, 2, 16], "float32")
+    SCRATCH["xt" + _k] = ("sbuf", [128, 12, 2, 16], "float32")
+    SCRATCH["nm" + _k] = ("sbuf", [128, 12, 16], "float32")
+for _n, _s, _d in (
+            ("v", [1024], "bfloat16"), ("y", [1024], "bfloat16"), ("sg", [1024], "bfloat16"), ("ab", [1024], "bfloat16"),
+            ("x17", [2, 68], "float32"), ("km", [68], "int32"), ("cc", [68], "int32"), ("par", [68], "int32"),
+            ("st", [68], "int32"), ("pos", [68], "bfloat16"), ("g1", [68], "bfloat16"), ("g2", [68], "bfloat16"),
+            ("mx", [72], "bfloat16"), ("mn", [72], "bfloat16"), ("a17", [NL, 17], "int32"), ("d1", [68], "float32"),
+            ("u", [68], "bfloat16"), ("w", [68], "bfloat16"), ("s2", [2, NL, 16], "int32"), ("zn", [64], "int32"),
+            ("si", [64], "int32"), ("q1", [2, NL, 16], "float16"), ("o1", [2, NL, 16, 16], "float16"),
+            ("ei", [64], "int32"), ("xx", [64], "int32"), ("eh", [64], "float32"), ("fh", [64], "float32"), ("v15", [64], "bfloat16"),
+            ("n32", [64], "float32"), ("az", [64], "int32"), ("sf", [64], "int32"), ("b2", [64], "int32"),
+            ("n2", [2, 64], "int32"), ("dl", [64], "bfloat16"), ("ii", [64], "bfloat16"), ("nb", [64], "bfloat16"),
+            ("ni", [64], "int32"), ("q2", [2, NL, 32], "float16"), ("o2", [2, NL, 16, 17], "float16"),
+            ("fi", [64], "int32"), ("nm", [NL, 16], "int32"),
+            ("tm", [NL, 2, 16], "float32"), ("tt", [NL, 2, 16], "float32"),
+            ("l0", [64], "uint16"),
+            ("m1", [128], "uint16"), ("m2", [128], "uint16"), ("le2", [128], "uint16"), ("le3", [128], "uint16"),
+            ("ls3", [128], "uint16"), ("yo2", [64], "float32"), ("yo3", [64], "float32"),
+            ("ly2", [64], "float32"), ("ly3", [64], "float32")):
+    SCRATCH[_n] = ("sbuf", [128, H] + _s, _d)
+SEMAPHORES = ["ldc", "lde", "lds", "out", "loc", "vec", "act", "pe", "gp", "as2"] + [
+    "%s%d" % (_a, _h) for _a in ("ae2", "ae3", "as3", "ay2", "ay3") for _h in range(H)]
+
+
+def rank_program(g, core, T, topo):
+    rank = T.rank_of(core)
+    if rank is None:
+        return
+    N = len(T.cores)
+    nxt = T.cores[(rank + 3) % N]
+    prv = T.cores[(rank + 7) % N]
+    opp = T.cores[(rank + 4) % N]
+    queue = {"v": g.vector, "s": g.scalar, "p": g.tensor, "g": g, "y": g.sync}
+    engsem = {"v": "vec", "s": "act", "p": "pe", "g": "gp"}
+    ops, lastw, rds, banks = [], {}, {}, {}
+
+    def op(eng, cost, fn, r=(), w=(), bank=(), sem=None, val=0, lat=0.0):
+        i = len(ops)
+        dep = set()
+        for k in r:
+            if k in lastw: dep.add(lastw[k])
+        for k in w:
+            if k in lastw: dep.add(lastw[k])
+            dep.update(rds.get(k, ()))
+        for b in bank:
+            dep.update(j for e, j in banks.setdefault(b, {}).items() if e != eng)
+            banks[b][eng] = i
+        dep.discard(i)
+        for k in r: rds.setdefault(k, []).append(i)
+        for k in w: lastw[k] = i; rds[k] = []
+        ops.append(dict(eng=eng, cost=cost, fn=fn, dep=dep, sem=sem, val=val, lat=lat))
+        return i
+
+    def V(elems, fn, r=(), w=(), bank=(), calls=1):
+        op("v", calls * max(64, elems) * CY, fn, r, w, bank)
+
+    def S(cycles, fn, r=(), w=(), bank=()):
+        op("s", cycles * CY, fn, r, w, bank)
+
+    def P(cycles, fn, r=(), w=(), bank=()):
+        op("p", cycles * PCY, fn, r, w, bank)
+
+    v, s, te = g.vector, g.scalar, g.tensor
+    B = lambda n, h: T[n][:, h]
+
+    def dma(eng, q, out, in_, sem, r=(), w=(), lat=2000.0, cost=60.0):
+        op(eng, cost, lambda: [(q.dma_start(out, in_), sem, 16)], r, w, sem=sem, val=16, lat=lat)
+
+    dma("y", g.sync, T.en[:], T.enz[:], "lde", w=["en"])
+    dma("s", g.scalar, T.su[:], T.subs[:], "lds", w=["su"])
+    dma("y", g.sync, T.ct[:], T.cont[:], "ldc", w=["ct"], lat=6000.0)
+
+    V(128, lambda: v.memset(T.one[:], 1.0), w=["one"])
+    op("g", 140, lambda: g.iota(T.pid[:], [[0, 1]], 0, 1), w=["pid"])
+    V(1, lambda: v.tensor_scalar(T.pbit[:], T.pid[:], 16, None, A.bitwise_and), ["pid"], ["pbit"])
+    V(1, lambda: v.tensor_scalar(T.modd[:], T.pbit[:], 1.0 / 16, None, A.mult), ["pbit"], ["modd"])
+    V(1, lambda: v.tensor_scalar(T.meven[:], T.pbit[:], -1.0 / 16, 1.0, A.mult, A.add), ["pbit"], ["meven"])
+    op("g", 380, lambda: g.affine_select(T.idf[:], T.one[:], [[-1, 128]], A.is_equal, 0.0, 0, 1), ["one"], ["idf"])
+    V(8, lambda: v.memset(T.g8a[:], 1.0), w=["g8a"])
+    op("g", 190, lambda: g.affine_select(T.g8b[:], T.g8a[:], [[-16, 8]], A.is_ge, 0.0, 0, 1), ["g8a"], ["g8b"])
+    op("g", 190, lambda: g.affine_select(T.g8c[:], T.g8b[:], [[16, 8]], A.is_ge, 0.0, 15, -1), ["g8b"], ["g8c"])
+
+    def initial(k, src):
+        xm, xt, nm = T["xm" + k], T["xt" + k], T["nm" + k]
+        V(192, lambda: v.tensor_scalar(xm[:, :, 0, :], T[src][:], T.meven[:], None, A.mult), [src, "meven"], ["xm0" + k])
+        V(192, lambda: v.tensor_scalar(xm[:, :, 1, :], T[src][:], T.modd[:], None, A.mult), [src, "modd"], ["xm1" + k])
+        V(384, lambda: v.transpose(xt[:], xm[:]) if False else v.transpose(T["xt" + k][:, :, :, :], T["xm" + k][:, :, :, :]),
+          ["xm0" + k, "xm1" + k], ["xt" + k])
+        V(384, lambda: v.tensor_tensor(nm[:], xt[:, :, 0, :], xt[:, :, 1, :], A.add), ["xt" + k], ["nm" + k])
+
+    def lists(dst, src3, rk, wk):
+        for c in range(NL):
+            V(16, lambda c=c: v.tensor_copy(dst[:, c:64:NL], src3[:, c, :]), rk, [(wk, c)])
+
+    initial("e", "en")
+    for h in range(H):
+        lists(T.m0[:, h, 0:64], T.nme[:, NL * h:NL * h + NL, :], ["nme"], ("m0l", h))
+        if h == 0:
+            initial("s", "su")
+        lists(B("l0", h), T.nms[:, NL * h:NL * h + NL, :], ["nms"], ("l0", h))
+        if h == 0:
+            for n, val in (("ip", 1.0), ("im", -1.0), ("i16th", 1.0 / 16), ("i2048", 2048.0), ("i16", 16.0), ("i32", 32.0),
+                           ("iph", 1.0), ("i8192", 8192.0), ("im256", -256.0)):
+                V(128, lambda n=n, val=val: v.tensor_scalar(T[n][:], T.idf[:], val, None, A.mult), ["idf"], [n])
+            for n, val in (("selc", 0.5), ("seld", 65536.0)):
+                V(80, lambda n=n: v.memset(T[n][:], 0.0), w=[n])
+                V(8, lambda n=n, val=val: v.tensor_scalar(T[n][:, 15:143:16], T.g8c[:], val, None, A.mult), ["g8c"], [n])
+            V(64, lambda: v.memset(T.kc8[:], 8.0), w=["kc8"])
+            for n, pat, base in (("krow", [[4096, 16], [0, NL]], 0), ("kkeep", [[0, NL], [256, 16]], -2048), ("kfill", [[0, NL], [256, 16]], 2048)):
+                op("g", 240, lambda n=n, pat=pat, base=base: g.iota(T[n][:], pat, base, 0, allow_small_or_imprecise_dtypes=True), w=[n])
+            for q in range(H):
+                V(136, lambda q=q: v.memset(B("x17", q)[:], 0.0), w=[("x17", q)])
+                V(72, lambda q=q: v.memset(B("mx", q)[:, 68:72], 0.0), w=[("mxpad", q)])
+                V(72, lambda q=q: v.memset(B("mn", q)[:, 68:72], 0.0), w=[("mnpad", q)])
+                V(72, lambda q=q: v.memset(B("a17", q)[:], 0), w=[("a17", q)])
+            for n, base, at, val in (("rk17", 0.0, (0,), BIG), ("mk17", 1.0, (0,), 0.0), ("rm17", 0.0, (15, 16), -1.0e6), ("rn17", 0.0, (15, 16), 1.0e6),
+                                     ("kw", 2128.0, (15,), -1968.0)):
+                V(68, lambda n=n, base=base: v.memset(T[n][:], base), w=[n])
+                for a in at:
+                    V(4, lambda n=n, a=a, val=val: v.memset(T[n][:, a::17], val), w=[n])
+            for n, base, at, val in (("mk16", 1.0, 0, 0.0), ("rm16", 0.0, 15, -1.0e6)):
+                V(64, lambda n=n, base=base: v.memset(T[n][:], base), w=[n])
+                V(4, lambda n=n, at=at, val=val: v.memset(T[n][:, at::16], val), w=[n])
+    for h in range(H):
+        V(64, lambda h=h: v.tensor_copy(T.m0[:, h, 64:128], T.nme[:, NL * h:NL * h + NL, :]), ["nme"], [("m0n", h)])
+    nloc = [0]
+
+    def remote(dst, out, in_, sem, r):
+        rid, pid = topo.addr(dst, core)
+        m = topo.mask(core, dst)
+        nloc[0] += len(topo.engines(core, dst))
+        op("g", 300, lambda: [(g.remote_dma(out, in_, T.sem[sem], T.sem.loc, pid, rid, m), None, 0)], r)
+
+    def arrive(sem, w, sends):
+        ne = len(topo.engines(core, nxt))
+        i = op("r", 0, None, (), w, sem=sem, val=ne, lat=2500.0)
+        ops[i]["dep"].add(sends)
+
+    remote(opp, T.ls2[:], T.m0[:], "as2", [(("m0l", h), c) for h in range(H) for c in range(NL)] + [("m0n", h) for h in range(H)])
+    arrive("as2", ["ls2"], len(ops) - 1)
+
+    dn = [0]
+    for t in range(1, R + 1):
+        for h in range(H):
+            b = lambda n: B(n, h)
+            K = lambda *n: [(x, h) for x in n]
+            pu, pE = T["pu%d" % ((t * H + h) % 2)], T["pe%d" % ((t * H + h) % 2)]
+            ub, eb = "pu%d" % ((t * H + h) % 2), "pe%d" % ((t * H + h) % 2)
+            ck = T.pck[:, h, :, :, :]
+            if t == 1:
+                el, e15, ek = T.m0[:, h, 0:64], T.m0[:, h, 60:64], [(("m0l", h), c) for c in range(NL)]
+                sl, sk = b("l0")[:, 0:64], [(("l0", h), c) for c in range(NL)]
+                en3, enk = T.nme[:, NL * h:NL * h + NL, :], ["nme"]
+                zn, znk = T.nms[:, NL * h:NL * h + NL, :], ["nms"]
+            else:
+                el, e15, ek = b("le%d" % t)[:, 0:64], b("le%d" % t)[:, 60:64], [("le%d" % t, h)]
+                en3, enk = b("le%d" % t)[:, 64:128], ek
+                if t == 2:
+                    sl, sk, zs = T.ls2[:, h, 0:64], ["ls2"], T.ls2[:, h, 64:128]
+                else:
+                    sl, sk, zs = b("ls3")[:, 0:64], K("ls3"), b("ls3")[:, 64:128]
+                zn, znk = b("zn")[:], K("zn")
+            gc = 80 + 1024 * 1.55
+            S(80 + 64 * 1.55, lambda y=b("v15"), l=e15: s.activation(y[:], T.ct[:].indirect(l), F.Copy), ["ct"] + ek, K("v15"))
+            for x, l, lk in (("y", sl, sk), ("v", el, ek)):
+                if (t, h, x) in ON_VECTOR:
+                    V(gc, lambda y=b(x), l=l: v.tensor_copy(y[:], T.ct[:].indirect(l)), ["ct"] + lk, K(x))
+                else:
+                    S(gc, lambda y=b(x), l=l: s.activation(y[:], T.ct[:].indirect(l), F.Copy), ["ct"] + lk, K(x))
+                if x == "y":
+                    ops[-1]["late"] = True
+
+            def vdiff(q, p, x):
+                m = te.matmul
+                m(p[:], T.ip[:], x[:, 512 * q:512 * q + 512], True, False)
+                if q == 0:
+                    return m(p[:], T.im[:], x[:, 64:576], False, True)
+                m(p[:, 0:448], T.im[:], x[:, 576:1024], False, False)
+                return m(p[:, 448:512], T.im[:], x[:, 0:64], False, True)
+
+            def ydiff(q, p, y, x):
+                te.matmul(p[:], T.ip[:], y[:, 512 * q:512 * q + 512], True, False)
+                for i in range(8):
+                    z = te.matmul(p[:, 64 * i:64 * i + 64], T.im[:], x[:], False, i == 7)
+                return z
+
+            def sums(p, sel, x, con):
+                for m in range(16):
+                    te.matmul(p, sel[:, 15 - m:143 - m], x[:, m:1024:16], m == 0, False)
+                return te.matmul(p, T.ip[:], con[:], False, True)
+
+            for kind in (1, 0):
+                for q in range(2):
+                    pn = "pdiff%d" % (dn[0] % 2); dn[0] += 1
+                    if kind == 0:
+                        P(1024, lambda q=q, p=T[pn], x=b("v"): vdiff(q, p, x), K("v") + ["ip", "im"], [pn], [pn])
+                        S(512, lambda q=q, p=T[pn], o=b("sg"): s.activation(o[:, 512 * q:512 * q + 512], p[:], F.Sign, bias=-0.5), [pn], [("sg%d" % q, h)], [pn])
+                    else:
+                        P(1024, lambda q=q, p=T[pn], y=b("y"), x=b("v15"): ydiff(q, p, y, x), K("v15", "y") + ["ip", "im"], [pn], [pn])
+                        S(512, lambda q=q, p=T[pn], o=b("ab"): s.activation(o[:, 512 * q:512 * q + 512], p[:], F.Abs), [pn], [("ab%d" % q, h)], [pn])
+            P(1088, lambda p=ck[:, 0, :, :], x=b("sg"): sums(p, T.selc, x, T.kc8), K("sg0", "sg1") + ["selc", "ip", "kc8"], K("pc"), ["pck"])
+            P(1088, lambda p=ck[:, 1, :, :], x=b("ab"): sums(p, T.seld, x, T.krow), K("ab0", "ab1") + ["seld", "ip", "krow"], K("pk"), ["pck"])
+            for c in range(NL):
+                S(64, lambda c=c, p=ck, x=b("x17"): s.activation(x[:, :, 17 * c:17 * c + 16], p[:, :, :, c], F.Copy), K("pc", "pk"), [("x17", h, c)], ["pck"])
+            x17k = [("x17", h)] + [("x17", h, c) for c in range(NL)]
+            V(64, lambda o=b("si"), x=en3: v.tensor_copy(o[:], x), enk, K("si"))
+            V(64, lambda o=b("s2"), x=b("si"): v.tensor_scalar(o[:, 0, :, :], x[:], 7, None, A.arith_shift_right), K("si"), K("s2h"))
+            V(64, lambda o=b("n2"), x=b("si"): v.tensor_scalar(o[:, 0, :], x[:], 127, None, A.bitwise_and), K("si"), K("n2h"))
+            V(128, lambda o=b("s2"), x=b("n2"): v.tensor_tensor(o[:, 1, :, :], x[:, 0, :], o[:, 0, :, :], A.add), K("n2h", "s2h"), K("s2l"))
+            if t > 1:
+                V(64, lambda o=b("zn"), x=zs: v.tensor_copy(o[:], x), sk, K("zn"))
+            V(68, lambda x=b("x17"), o=b("cc"): v.tensor_tensor_scan(o[:], T.mk17[:], x[:, 0, :], 0.0, A.mult, A.add), x17k + ["mk17"], K("cc"))
+            V(68, lambda x=b("x17"), o=b("km"): v.tensor_tensor_scan(o[:], T.rk17[:], x[:, 1, :], 0.0, A.add, A.min), x17k + ["rk17"], K("km"))
+            V(68, lambda x=b("cc"), o=b("par"): v.tensor_scalar(o[:], x[:], 1, None, A.bitwise_and), K("cc"), K("par"))
+            V(68, lambda x=b("par"), o=b("st"): v.tensor_scalar(o[:], x[:], -8192.0, 4096.0, A.mult, A.add), K("par"), K("st"))
+            V(4, lambda x=b("km"), o=b("st"): v.tensor_scalar(o[:, 0::17], x[:, 15::17], 61440, None, A.bitwise_and), K("km"), K("st"))
+            V(68, lambda x=b("st"), o=b("pos"): v.tensor_tensor_scan(o[:], T.mk17[:], x[:], 0.0, A.mult, A.add), K("st") + ["mk17"], K("pos"))
+            V(68, lambda x=b("pos"), o=b("mx"): v.tensor_tensor_scan(o[:, 67::-1], T.rm17[:, ::-1], x[:, ::-1], 0.0, A.add, A.max), K("pos") + ["rm17"], K("mx"))
+            V(68, lambda x=b("pos"), o=b("mn"): v.tensor_tensor_scan(o[:, 67::-1], T.rn17[:, ::-1], x[:, ::-1], 0.0, A.add, A.min), K("pos") + ["rn17"], K("mn"))
+            S(68, lambda x=b("pos"), o=b("g1"): s.activation(o[:], x[:], F.Sign, bias=63488.0, scale=-1.0), K("pos"), K("g1"))
+            S(68, lambda x=b("pos"), o=b("g2"): s.activation(o[:], x[:], F.Sign, bias=-2048.0, scale=-1.0), K("pos"), K("g2"))
+            S(68, lambda x=b("x17"), o=b("w"): s.activation(o[:], x[:, 0, :], F.Sign, bias=-9.5), x17k, K("w"))
+            if t > 1:
+                V(136, lambda x=b("x17"), o=b("d1"), a=b("a17"): v.tensor_tensor(o[:], x[:, 0, :], a[:], A.subtract), x17k + K("a17"), K("d1"))
+            dk, dx = (K("d1"), b("d1")) if t > 1 else (x17k, b("x17")[:, 0, :])
+            S(68, lambda x=dx, o=b("u"): s.activation(o[:], x[:], F.Sign, bias=5.5, scale=-1.0), dk, K("u"))
+
+            def usum(p, h):
+                o = p[:, 0, :, 0:17]
+                te.matmul(o, T.ip[:], T.kw[:], True, False)
+                te.matmul(o, T.i16[:], B("w", h)[:], False, False)
+                te.matmul(o, T.i32[:], B("u", h)[:], False, False)
+                te.matmul(o, T.i16th[:], B("pos", h)[:], False, False)
+                te.matmul(o, T.i2048[:], B("g1", h)[:], False, False)
+                te.matmul(o, T.i2048[:], B("g2", h)[:], False, False)
+                te.matmul(o, T.im[:], B("mx", h)[:, 0:68], False, False)
+                te.matmul(o, T.ip[:], B("mx", h)[:, 1:69], False, False)
+                te.matmul(o, T.ip[:], B("mn", h)[:, 0:68], False, False)
+                return te.matmul(o, T.im[:], B("mn", h)[:, 1:69], False, True)
+            P(680, lambda p=pu, h=h: usum(p, h), K("pos", "g1", "g2", "u", "w", "mx", "mn", "mxpad", "mnpad") + ["ip", "im", "i16th", "i16", "i32", "i2048", "kw"], ["U" + ub], [ub])
+            for a, sk2 in ((0, "s2h"), (1, "s2l")):
+                V(64, lambda a=a, o=b("q1"), x=b("s2"), p=pu: v.tensor_tensor(o[:, a, :, :], x[:, a, :, :], p[:, 0, :, 0:16], A.add), K(sk2) + ["U" + ub], K("q1%d" % a), [ub])
+            for p_ in range(16):
+                V(64, lambda p_=p_, o=b("o1"), x=b("q1"): v.tensor_scalar(o[:, :, :, p_, :], x[:], 256.0 * p_ - 2048.0, 256.0 * p_ - 1792.0, A.max, A.min), K("q10", "q11"), [("o1", h, p_)])
+
+            def picked(p, q, o, n, f):
+                for k in range(n):
+                    z = te.matmul(p[:, q:q + 2, :, 8 * f:8 * f + 8], T.iph[:], o[:, :, :, 8 * f:8 * f + 8, k], k == 0, k == n - 1)
+                return z
+            for f in range(2):
+                P(1024, lambda p=pE, o=b("o1"), f=f: picked(p, 0, o, 16, f), [("o1", h, p_) for p_ in range(8 * f, 8 * f + 8)] + ["iph"], ["E%d" % f + eb], [eb])
+            V(64, lambda o=b("eh"), p=pE: v.tensor_scalar(o[:], p[:, 0, :, :], 127.0, None, A.mult), ["E0" + eb, "E1" + eb], K("eh"), [eb])
+            V(64, lambda o=b("ei"), x=b("eh"), p=pE: v.tensor_tensor(o[:], x[:], p[:, 1, :, :], A.add), ["E0" + eb, "E1" + eb] + K("eh"), K("ei"), [eb])
+            V(64, lambda o=b("xx"), x=b("ei"): v.tensor_scalar(o[:], x[:], 16383, None, A.bitwise_and), K("ei"), K("xx"))
+            pw = T.pw
+            c0 = 2 * h
+            V(64, lambda x=b("xx"), o=b("dl"): v.tensor_scalar(o[:], x[:], 12288.0, None, A.is_ge), K("xx"), K("dl"))
+            V(64, lambda x=b("dl"), o=b("ii"): v.tensor_tensor_scan(o[:], T.mk16[:], x[:], 0.0, A.mult, A.add), K("dl") + ["mk16"], K("ii"))
+            V(64, lambda x=b("ii"), o=b("nb"): v.tensor_tensor_scan(o[:, ::-1], T.rm16[:, ::-1], x[:, ::-1], 0.0, A.add, A.max), K("ii") + ["rm16"], K("nb"))
+
+            def tsum(p, h):
+                o = p[:, 0, :, 20:36]
+                te.matmul(o, T.ip[:], T.kkeep[:], True, False)
+                te.matmul(o, T.i8192[:], B("dl", h)[:], False, False)
+                te.matmul(o, T.im256[:], B("ii", h)[:], False, True)
+                o = p[:, 0, :, 36:52]
+                te.matmul(o, T.ip[:], T.kfill[:], True, False)
+                return te.matmul(o, T.im256[:], B("nb", h)[:], False, True)
+            P(320, lambda p=pu, h=h: tsum(p, h), K("dl", "ii", "nb") + ["i8192", "im256", "ip", "kkeep", "kfill"], ["T" + ub], [ub])
+            V(64, lambda x=b("xx"), c0=c0: v.tensor_scalar(pw[:, c0, :], x[:], -8192.0, 0.0, A.add, A.max), K("xx"), [("pw", c0)])
+            V(64, lambda x=b("xx"), o=b("n32"): v.tensor_scalar(o[:], x[:], 4096.0, 32.0, A.is_lt, A.mult), K("xx"), K("n32"))
+            V(64, lambda x=b("xx"), c0=c0, t=t: v.tensor_scalar(pw[:, c0 + 1, :], x[:], 8192.0, 77.0 * t, A.is_ge, A.mult), K("xx"), [("pw", c0 + 1)])
+            V(64, lambda x=b("xx"), c0=c0: v.tensor_tensor(pw[:, c0 + 1, :], x[:], pw[:, c0 + 1, :], A.add), K("xx"), [("pw", c0 + 1)])
+            V(64, lambda x=b("n32"), c0=c0: v.tensor_tensor(pw[:, c0, :], x[:], pw[:, c0, :], A.add), K("n32"), [("pw", c0)])
+            V(64, lambda x=zn, o=b("az"), c0=c0: v.tensor_tensor(o[:], x, pw[:, c0, :], A.mult), znk + [("pw", c0)], K("az"))
+            V(64, lambda x=b("az"), o=b("sf"): v.tensor_scalar(o[:], x[:], 5, 4095, A.arith_shift_right, A.bitwise_and), K("az"), K("sf"))
+            V(64, lambda x=b("sf"), o=b("b2"), c0=c0: v.tensor_tensor(o[:], x[:], pw[:, c0 + 1, :], A.add), K("sf") + [("pw", c0 + 1)], K("b2"))
+            V(64, lambda x=b("b2"), o=b("n2"): v.tensor_scalar(o[:, 0, :], x[:], 7, 31, A.arith_shift_right, A.bitwise_and), K("b2"), K("n2h"))
+            V(64, lambda x=b("b2"), o=b("n2"): v.tensor_scalar(o[:, 1, :], x[:], 127, None, A.bitwise_and), K("b2"), K("n2l"))
+            for a, sk2 in ((0, "s2h"), (1, "s2l")):
+                V(64, lambda a=a, o=b("q2"), x=b("s2"), p=pu: v.tensor_tensor(o[:, a, :, 16:32], x[:, a, :, :], p[:, 0, :, 36:52], A.add), K(sk2) + ["T" + ub], K("q2b%d" % a), [ub])
+            V(64, lambda x=b("n2"), p=pu, c0=c0: v.tensor_tensor(pw[:, c0, :], x[:, 0, :], p[:, 0, :, 20:36], A.add), K("n2h") + ["T" + ub], [("pw", c0)], [ub])
+            V(64, lambda x=b("n2"), o=b("q2"), c0=c0: v.tensor_tensor(o[:, 1, :, 0:16], x[:, 1, :], pw[:, c0, :], A.add), K("n2l") + [("pw", c0)], K("q2a1"))
+            V(64, lambda o=b("q2"), c0=c0: v.tensor_copy(o[:, 0, :, 0:16], pw[:, c0, :]), [("pw", c0)], K("q2a0"))
+            for i in range(16):
+                V(68, lambda i=i, o=b("o2"), x=b("q2"): v.tensor_scalar(o[:, :, :, i, :], x[:, :, :, i:i + 17], 256.0 * i - 2048.0, 256.0 * i - 1792.0, A.max, A.min), K("q2a0", "q2a1", "q2b0", "q2b1"), [("o2", h, i)])
+            for f in range(2):
+                P(1088, lambda p=pE, o=b("o2"), f=f: picked(p, 2, o, 17, f), [("o2", h, i) for i in range(8 * f, 8 * f + 8)] + ["iph"], ["R%d" % f + eb], [eb])
+            V(64, lambda o=b("fh"), p=pE: v.tensor_scalar(o[:], p[:, 2, :, :], 127.0, None, A.mult), ["R0" + eb, "R1" + eb], K("fh"), [eb])
+            V(64, lambda o=b("fi"), x=b("fh"), p=pE: v.tensor_tensor(o[:], x[:], p[:, 3, :, :], A.add), ["R0" + eb, "R1" + eb] + K("fh"), K("fi"), [eb])
+            V(64, lambda o=b("nm"), x=b("fi"): v.tensor_scalar(o[:], x[:], 4095, None, A.bitwise_and), K("fi"), K("nm"))
+            if t < R:
+                m = b("m%d" % t)
+                lists(m[:, 0:64], b("nm"), K("nm"), ("m%dl" % t, h))
+                V(64, lambda m=m, x=b("nm"): v.tensor_copy(m[:, 64:128], x[:]), K("nm"), [("m%dn" % t, h)])
+                mk = [(("m%dl" % t, h), c) for c in range(NL)] + [("m%dn" % t, h)]
+                remote(nxt, b("le%d" % (t + 1))[:], m[:], "ae%d%d" % (t + 1, h), mk)
+                arrive("ae%d%d" % (t + 1, h), K("le%d" % (t + 1)), len(ops) - 1)
+                if t + 2 <= R:
+                    remote(prv, b("ls%d" % (t + 2))[:], m[:], "as%d%d" % (t + 2, h), mk)
+                    arrive("as%d%d" % (t + 2, h), K("ls%d" % (t + 2)), len(ops) - 1)
+                V(64, lambda x=b("nb"), o=b("ni"): v.tensor_copy(o[:], x[:]), K("nb"), K("ni"))
+                V(64, lambda x=b("ni"), o=b("a17"): v.tensor_scalar(o[:, :, 0:16], x[:], 1, None, A.bitwise_and), K("ni"), K("a17"))
+            if t >= R - 1:
+                V(64, lambda x=b("nm"), o=b("tm"): v.tensor_scalar(o[:, :, 0, :], x[:], T.meven[:], None, A.mult), K("nm") + ["meven"], K("tm0"))
+                V(64, lambda x=b("nm"), o=b("tm"): v.tensor_scalar(o[:, :, 1, :], x[:], T.modd[:], None, A.mult), K("nm") + ["modd"], K("tm1"))
+                V(128, lambda x=b("tm"), o=b("tt"): v.transpose(o[:], x[:]), K("tm0", "tm1"), K("tt"))
+                V(128, lambda x=b("tt"), o=b("yo%d" % t): v.tensor_tensor(o[:], x[:, :, 0, :], x[:, :, 1, :], A.add), K("tt"), K("yo%d" % t))
+                remote(nxt if t == R else prv, b("ly%d" % t)[:], b("yo%d" % t)[:], "ay%d%d" % (t, h), K("yo%d" % t))
+                arrive("ay%d%d" % (t, h), K("ly%d" % t), len(ops) - 1)
+                y = T.yenz if t == R else T.ysub
+                op("y", 60, lambda y=y, x=b("ly%d" % t), h=h: [(g.sync.dma_start(y[:, 64 * h:64 * h + 64], x[:]), "out", 16)], K("ly%d" % t))
+
+    WAKE = 60.0
+    n = len(ops)
+    succ = [[] for i in range(n)]
+    for i, o in enumerate(ops):
+        for d in o["dep"]: succ[d].append(i)
+        o["pr"] = i + (LATE if o.get("late") else 0)
+    rank_of_op = sorted(range(n), key=lambda i: ops[i]["pr"])
+
+    def schedule(known):
+        left = [len(o["dep"]) for o in ops]
+        ready = [0.0] * n
+        free, order, cand = {}, [], {}
+        urgent = {}
+        if known:
+            for i in rank_of_op: urgent.setdefault(ops[i]["eng"], []).append(i)
+        out = set()
+        end = 0.0
+        for i in range(n):
+            if not left[i]: cand.setdefault(ops[i]["eng"], []).append(i)
+        while True:
+            best = None
+            for e, c in cand.items():
+                if not c: continue
+                f = free.get(e, 0.0) if e != "r" else 0.0
+                starts = []
+                for i in c:
+                    st = max(ready[i], f)
+                    if known and ops[i]["cost"] > HOLD:
+                        lim = st + AHEAD * ops[i]["cost"]
+                        for j in urgent[e]:
+                            if ops[j]["pr"] >= ops[i]["pr"]: break
+                            if j not in out and left[j] and st < known[j] < lim: st = known[j] + 1.0
+                    starts.append((st, i))
+                lo = min(starts)[0]
+                pr, st, i = min((ops[i]["pr"], st, i) for st, i in starts if st <= lo + 20.0)
+                key = (st, i)
+                if best is None or key < best[0]: best = (key, e, i)
+            if best is None: break
+            (st, _), e, i = best
+            cand[e].remove(i)
+            out.add(i)
+            o = ops[i]
+            free[e] = st + o["cost"]
+            fin = st + o["cost"] + o["lat"]
+            end = max(end, fin)
+            order.append(i)
+            for j in succ[i]:
+                ready[j] = max(ready[j], fin + WAKE)
+                left[j] -= 1
+                if not left[j]: cand.setdefault(ops[j]["eng"], []).append(j)
+        return end, order, ready
+
+    best, known = None, None
+    for k in range(PASSES):
+        end, order, known = schedule(known)
+        if best is None or end < best[0]: best = (end, order)
+    order = best[1]
+
+    count, done, waited = {}, {}, {}
+    ndma = [0]
+    for i in order:
+        o = ops[i]
+        e = o["eng"]
+        if e == "r":
+            done[i] = (o["sem"], o["val"])
+            continue
+        need = {}
+        for d in o["dep"]:
+            sm, val = done[d]
+            need[sm] = max(need.get(sm, 0), val)
+        for sm in sorted(need):
+            if waited.get((e, sm), 0) < need[sm]:
+                queue[e].wait_ge(T.sem[sm], need[sm])
+                waited[(e, sm)] = need[sm]
+        x = o["fn"]()
+        if isinstance(x, list):
+            ins, sm, inc = x[0]
+            if sm is not None:
+                ins.then_inc(T.sem[sm], inc)
+                if sm == "out": ndma[0] += inc
+            done[i] = (sm, o["val"])
+            if sm is None: done[i] = ("loc", 0)
+        else:
+            sm = engsem[e]
+            x.then_inc(T.sem[sm], 1)
+            count[sm] = count.get(sm, 0) + 1
+            done[i] = (sm, count[sm])
+    g.sync.wait_ge(T.sem.out, ndma[0])
+    g.wait_ge(T.sem.loc, nloc[0])
+    for sm in count:
+        g.wait_ge(T.sem[sm], count[sm])

@@ -1,15 +1,22 @@
 from concourse.bass import DstId, RemoteDMATransfer
 from concourse.mybir import dt, AluOpType as A, ActivationFunctionType as F
 
-H = 3
-NL = 4
+H = 2
+NL = 12 // H
+W, W17 = 16 * NL, 17 * NL
+NV = 16 * W
+RP = 8 if NL <= 4 else 4
+NP, PC = 16 // RP, RP * W
 R = 3
-CY = 0.83
-PCY = 0.42
+CY, VO, SO, PCY = 0.83, 50.0, 65.0, 0.42
+LATE, HOLD, AHEAD, PASSES, WAKE, RLAT = 100, 400.0, 0.8, 4, 60.0, 2500.0
 BIG = 1.0e9
-LATE, HOLD, AHEAD, PASSES = 100, 400.0, 0.8, 4
-ON_VECTOR = ((1, 0, "v"),)
+CKS = 4 if NL <= 4 else 2
+NDIFF = 4
 
+IDENT = (("ip", 1.0, "bfloat16"), ("im", -1.0, "bfloat16"), ("i16th", 1.0 / 16, "bfloat16"), ("i2048", 2048.0, "bfloat16"),
+         ("i16", 16.0, "bfloat16"), ("i32", 32.0, "bfloat16"), ("i4", 4.0, "bfloat16"), ("i8192", 8192.0, "bfloat16"),
+         ("im256", -256.0, "bfloat16"), ("iph", 1.0, "float16"), ("i127h", 127.0, "float16"))
 SCRATCH = {
     "ct": ("sbuf", [128, 4096], "bfloat16"),
     "en": ("sbuf", [128, 192], "int32"), "su": ("sbuf", [128, 192], "int32"),
@@ -18,47 +25,44 @@ SCRATCH = {
     "pid": ("sbuf", [128, 1], "int32"), "pbit": ("sbuf", [128, 1], "int32"),
     "modd": ("sbuf", [128, 1], "float32"), "meven": ("sbuf", [128, 1], "float32"),
     "selc": ("sbuf", [128, 160], "bfloat16"), "seld": ("sbuf", [128, 160], "bfloat16"),
-    "ip": ("sbuf", [128, 128], "bfloat16"), "im": ("sbuf", [128, 128], "bfloat16"),
-    "i16th": ("sbuf", [128, 128], "bfloat16"), "i8192": ("sbuf", [128, 128], "bfloat16"),
-    "i2048": ("sbuf", [128, 128], "bfloat16"), "i16": ("sbuf", [128, 128], "bfloat16"), "i32": ("sbuf", [128, 128], "bfloat16"),
-    "im256": ("sbuf", [128, 128], "bfloat16"), "iph": ("sbuf", [128, 128], "float16"),
-    "kc8": ("sbuf", [128, 64], "bfloat16"), "krow": ("sbuf", [128, 64], "bfloat16"),
-    "kw": ("sbuf", [128, 68], "bfloat16"),
-    "kkeep": ("sbuf", [128, 64], "bfloat16"), "kfill": ("sbuf", [128, 64], "bfloat16"),
-    "mk17": ("sbuf", [128, 68], "float32"), "rk17": ("sbuf", [128, 68], "float32"),
-    "rm17": ("sbuf", [128, 68], "float32"), "rn17": ("sbuf", [128, 68], "float32"),
-    "mk16": ("sbuf", [128, 64], "float32"), "rm16": ("sbuf", [128, 64], "float32"),
-    "m0": ("sbuf", [128, H, 128], "uint16"), "ls2": ("sbuf", [128, H, 128], "uint16"),
-    "pdiff0": ("psum", [128, 512], "float32"), "pdiff1": ("psum", [128, 512], "float32"),
-    "pck": ("psum", [128, 4, 2, 16, NL], "float32"),
-    "pu0": ("psum", [128, 2, NL, 64], "float32"), "pu1": ("psum", [128, 2, NL, 64], "float32"),
-    "pe0": ("psum", [128, 8, NL, 16], "float32"), "pe1": ("psum", [128, 8, NL, 16], "float32"),
-    "pw": ("psum", [128, 8, 64], "float32"),
+    "kc8": ("sbuf", [128, W], "bfloat16"), "krow": ("sbuf", [128, W], "bfloat16"),
+    "kw": ("sbuf", [128, W17], "bfloat16"), "tg17": ("sbuf", [128, W17], "float32"),
+    "kkeep": ("sbuf", [128, W], "bfloat16"), "kfill": ("sbuf", [128, W], "bfloat16"),
+    "mk17": ("sbuf", [128, W17], "float32"), "rk17": ("sbuf", [128, W17], "float32"),
+    "rm17": ("sbuf", [128, W17], "float32"), "rn17": ("sbuf", [128, W17], "float32"),
+    "mk16": ("sbuf", [128, W], "float32"), "rm16": ("sbuf", [128, W], "float32"),
+    "m0l": ("sbuf", [128, H, W], "uint16"), "ls2": ("sbuf", [128, H, W], "uint16"), "lsn2": ("sbuf", [128, 12, 16], "int32"),
+    "nme": ("sbuf", [128, 12, 16], "int32"), "nms": ("sbuf", [128, 12, 16], "int32"),
+    "pck": ("psum", [128, CKS, 2, 16, 16 // CKS], "float32"),
+    "pe0": ("psum", [128, 8, 64], "float32"), "pe1": ("psum", [128, 8, 64], "float32"),
+    "pw": ("psum", [128, 2 * CKS, 256 // CKS], "float32"),
 }
+for _q in range(NDIFF):
+    SCRATCH["pd%d" % _q] = ("psum", [128, 512], "float32")
+for _n, _v, _d in IDENT:
+    SCRATCH[_n] = ("sbuf", [128, 128], _d)
 for _k in ("e", "s"):
     SCRATCH["xm" + _k] = ("sbuf", [128, 12, 2, 16], "float32")
     SCRATCH["xt" + _k] = ("sbuf", [128, 12, 2, 16], "float32")
-    SCRATCH["nm" + _k] = ("sbuf", [128, 12, 16], "float32")
 for _n, _s, _d in (
-            ("v", [1024], "bfloat16"), ("y", [1024], "bfloat16"), ("sg", [1024], "bfloat16"), ("ab", [1024], "bfloat16"),
-            ("x17", [2, 68], "float32"), ("km", [68], "int32"), ("cc", [68], "int32"), ("par", [68], "int32"),
-            ("st", [68], "int32"), ("pos", [68], "bfloat16"), ("g1", [68], "bfloat16"), ("g2", [68], "bfloat16"),
-            ("mx", [72], "bfloat16"), ("mn", [72], "bfloat16"), ("a17", [NL, 17], "int32"), ("d1", [68], "float32"),
-            ("u", [68], "bfloat16"), ("w", [68], "bfloat16"), ("s2", [2, NL, 16], "int32"), ("zn", [64], "int32"),
-            ("si", [64], "int32"), ("q1", [2, NL, 16], "float16"), ("o1", [2, NL, 16, 16], "float16"),
-            ("ei", [64], "int32"), ("xx", [64], "int32"), ("eh", [64], "float32"), ("fh", [64], "float32"), ("v15", [64], "bfloat16"),
-            ("n32", [64], "float32"), ("az", [64], "int32"), ("sf", [64], "int32"), ("b2", [64], "int32"),
-            ("n2", [2, 64], "int32"), ("dl", [64], "bfloat16"), ("ii", [64], "bfloat16"), ("nb", [64], "bfloat16"),
-            ("ni", [64], "int32"), ("q2", [2, NL, 32], "float16"), ("o2", [2, NL, 16, 17], "float16"),
-            ("fi", [64], "int32"), ("nm", [NL, 16], "int32"),
-            ("tm", [NL, 2, 16], "float32"), ("tt", [NL, 2, 16], "float32"),
-            ("l0", [64], "uint16"),
-            ("m1", [128], "uint16"), ("m2", [128], "uint16"), ("le2", [128], "uint16"), ("le3", [128], "uint16"),
-            ("ls3", [128], "uint16"), ("yo2", [64], "float32"), ("yo3", [64], "float32"),
-            ("ly2", [64], "float32"), ("ly3", [64], "float32")):
+        ("v", [NV], "bfloat16"), ("y", [NV], "bfloat16"), ("sg", [NV], "bfloat16"), ("ab", [NV], "bfloat16"), ("v15", [W], "bfloat16"),
+        ("x17", [2, W17], "float32"), ("km", [W17], "int32"), ("cc", [W17], "int32"), ("par", [W17], "int32"),
+        ("st", [W17], "int32"), ("pb", [W17], "int32"), ("od", [W17], "bfloat16"), ("pos", [W17], "bfloat16"),
+        ("g1", [W17], "bfloat16"), ("g2", [W17], "bfloat16"), ("mx", [W17 + 4], "bfloat16"), ("mn", [W17 + 4], "bfloat16"),
+        ("a17", [NL, 17], "int32"), ("d1", [W17], "float32"), ("u", [W17], "bfloat16"), ("w", [W17], "bfloat16"),
+        ("s2", [2, NL, 16], "int32"), ("q1", [2, NL, 16], "float32"), ("qx", [2, NL, 8], "float32"), ("qp", [2, NL, 2, 8], "float16"),
+        ("o1", [2, NL, 8, 2, 8], "float16"), ("ei", [W], "int32"), ("xx", [W], "int32"), ("n32", [W], "float32"),
+        ("az", [W], "int32"), ("sf", [W], "int32"), ("b2", [W], "int32"), ("n2", [2, W], "int32"), ("sl", [W], "int32"),
+        ("dl", [W], "bfloat16"), ("ii", [W], "bfloat16"), ("nb", [W], "bfloat16"), ("ni", [W], "int32"),
+        ("q2", [2, NL, 32], "float16"), ("o2", [2, NL, 16, 17], "float16"), ("fi", [W], "int32"),
+        ("nm1", [NL, 16], "int32"), ("nm2", [NL, 16], "int32"), ("nm3", [NL, 16], "int32"),
+        ("tm", [NL, 2, 16], "float32"), ("tt", [NL, 2, 16], "float32"), ("l0", [W], "uint16"),
+        ("ml1", [W], "uint16"), ("ml2", [W], "uint16"), ("le2", [W], "uint16"), ("le3", [W], "uint16"), ("ls3", [W], "uint16"),
+        ("len2", [NL, 16], "int32"), ("len3", [NL, 16], "int32"), ("lsn3", [NL, 16], "int32"),
+        ("yo2", [W], "float32"), ("yo3", [W], "float32"), ("ly2", [W], "float32"), ("ly3", [W], "float32")):
     SCRATCH[_n] = ("sbuf", [128, H] + _s, _d)
-SEMAPHORES = ["ldc", "lde", "lds", "out", "loc", "vec", "act", "pe", "gp", "as2"] + [
-    "%s%d" % (_a, _h) for _a in ("ae2", "ae3", "as3", "ay2", "ay3") for _h in range(H)]
+SEMAPHORES = ["ldc", "lde", "lds", "out", "loc", "vec", "act", "pe", "gp", "ls2", "lsn2"] + [
+    "%s%d" % (_a, _h) for _a in ("le2", "le3", "ls3", "len2", "len3", "lsn3", "ly2", "ly3") for _h in range(H)]
 
 
 def rank_program(g, core, T, topo):
@@ -90,30 +94,31 @@ def rank_program(g, core, T, topo):
         ops.append(dict(eng=eng, cost=cost, fn=fn, dep=dep, sem=sem, val=val, lat=lat))
         return i
 
-    def V(elems, fn, r=(), w=(), bank=(), calls=1):
-        op("v", calls * max(64, elems) * CY, fn, r, w, bank)
+    def V(n, fn, r=(), w=(), bank=()):
+        op("v", VO + n * CY, fn, r, w, bank)
 
-    def S(cycles, fn, r=(), w=(), bank=()):
-        op("s", cycles * CY, fn, r, w, bank)
+    def S(n, fn, r=(), w=(), bank=()):
+        op("s", SO + n * CY, fn, r, w, bank)
 
-    def P(cycles, fn, r=(), w=(), bank=()):
-        op("p", cycles * PCY, fn, r, w, bank)
+    def P(n, fn, r=(), w=(), bank=()):
+        op("p", n * PCY, fn, r, w, bank)
 
     v, s, te = g.vector, g.scalar, g.tensor
     B = lambda n, h: T[n][:, h]
+    ts, tt, scan, act, mm = v.tensor_scalar, v.tensor_tensor, v.tensor_tensor_scan, s.activation, te.matmul
 
-    def dma(eng, q, out, in_, sem, r=(), w=(), lat=2000.0, cost=60.0):
-        op(eng, cost, lambda: [(q.dma_start(out, in_), sem, 16)], r, w, sem=sem, val=16, lat=lat)
+    def dma(eng, q, out, in_, sem, w, lat):
+        op(eng, 60.0, lambda: [(q.dma_start(out, in_), sem, 16)], (), w, sem=sem, val=16, lat=lat)
 
-    dma("y", g.sync, T.en[:], T.enz[:], "lde", w=["en"])
-    dma("s", g.scalar, T.su[:], T.subs[:], "lds", w=["su"])
-    dma("y", g.sync, T.ct[:], T.cont[:], "ldc", w=["ct"], lat=6000.0)
+    dma("y", g.sync, T.en[:], T.enz[:], "lde", ["en"], 2000.0)
+    dma("s", g.scalar, T.su[:], T.subs[:], "lds", ["su"], 2000.0)
+    dma("y", g.sync, T.ct[:], T.cont[:], "ldc", ["ct"], 6000.0)
 
     V(128, lambda: v.memset(T.one[:], 1.0), w=["one"])
     op("g", 140, lambda: g.iota(T.pid[:], [[0, 1]], 0, 1), w=["pid"])
-    V(1, lambda: v.tensor_scalar(T.pbit[:], T.pid[:], 16, None, A.bitwise_and), ["pid"], ["pbit"])
-    V(1, lambda: v.tensor_scalar(T.modd[:], T.pbit[:], 1.0 / 16, None, A.mult), ["pbit"], ["modd"])
-    V(1, lambda: v.tensor_scalar(T.meven[:], T.pbit[:], -1.0 / 16, 1.0, A.mult, A.add), ["pbit"], ["meven"])
+    V(1, lambda: ts(T.pbit[:], T.pid[:], 16, None, A.bitwise_and), ["pid"], ["pbit"])
+    V(1, lambda: ts(T.modd[:], T.pbit[:], 1.0 / 16, None, A.mult), ["pbit"], ["modd"])
+    V(1, lambda: ts(T.meven[:], T.pbit[:], -1.0 / 16, 1.0, A.mult, A.add), ["pbit"], ["meven"])
     op("g", 380, lambda: g.affine_select(T.idf[:], T.one[:], [[-1, 128]], A.is_equal, 0.0, 0, 1), ["one"], ["idf"])
     V(8, lambda: v.memset(T.g8a[:], 1.0), w=["g8a"])
     op("g", 190, lambda: g.affine_select(T.g8b[:], T.g8a[:], [[-16, 8]], A.is_ge, 0.0, 0, 1), ["g8a"], ["g8b"])
@@ -121,251 +126,239 @@ def rank_program(g, core, T, topo):
 
     def initial(k, src):
         xm, xt, nm = T["xm" + k], T["xt" + k], T["nm" + k]
-        V(192, lambda: v.tensor_scalar(xm[:, :, 0, :], T[src][:], T.meven[:], None, A.mult), [src, "meven"], ["xm0" + k])
-        V(192, lambda: v.tensor_scalar(xm[:, :, 1, :], T[src][:], T.modd[:], None, A.mult), [src, "modd"], ["xm1" + k])
-        V(384, lambda: v.transpose(xt[:], xm[:]) if False else v.transpose(T["xt" + k][:, :, :, :], T["xm" + k][:, :, :, :]),
-          ["xm0" + k, "xm1" + k], ["xt" + k])
-        V(384, lambda: v.tensor_tensor(nm[:], xt[:, :, 0, :], xt[:, :, 1, :], A.add), ["xt" + k], ["nm" + k])
+        V(192, lambda: ts(xm[:, :, 0, :], T[src][:], T.meven[:], None, A.mult), [src, "meven"], ["xm0" + k])
+        V(192, lambda: ts(xm[:, :, 1, :], T[src][:], T.modd[:], None, A.mult), [src, "modd"], ["xm1" + k])
+        V(384, lambda: v.transpose(xt[:, :, :, :], xm[:, :, :, :]), ["xm0" + k, "xm1" + k], ["xt" + k])
+        V(384, lambda: tt(nm[:], xt[:, :, 0, :], xt[:, :, 1, :], A.add), ["xt" + k], ["nm" + k])
 
     def lists(dst, src3, rk, wk):
         for c in range(NL):
-            V(16, lambda c=c: v.tensor_copy(dst[:, c:64:NL], src3[:, c, :]), rk, [(wk, c)])
+            V(16, lambda c=c: v.tensor_copy(dst[:, c:W:NL], src3[:, c, :]), rk, [(wk, c)])
 
     initial("e", "en")
     for h in range(H):
-        lists(T.m0[:, h, 0:64], T.nme[:, NL * h:NL * h + NL, :], ["nme"], ("m0l", h))
+        lists(T.m0l[:, h], T.nme[:, NL * h:NL * h + NL, :], ["nme"], ("m0l", h))
         if h == 0:
             initial("s", "su")
         lists(B("l0", h), T.nms[:, NL * h:NL * h + NL, :], ["nms"], ("l0", h))
         if h == 0:
-            for n, val in (("ip", 1.0), ("im", -1.0), ("i16th", 1.0 / 16), ("i2048", 2048.0), ("i16", 16.0), ("i32", 32.0),
-                           ("iph", 1.0), ("i8192", 8192.0), ("im256", -256.0)):
-                V(128, lambda n=n, val=val: v.tensor_scalar(T[n][:], T.idf[:], val, None, A.mult), ["idf"], [n])
+            for n, val, d in IDENT:
+                if d == "float16":
+                    V(128, lambda n=n, val=val: ts(T[n][:], T.idf[:], val, None, A.mult), ["idf"], [n])
+                else:
+                    S(128, lambda n=n, val=val: act(T[n][:], T.idf[:], F.Copy, scale=val), ["idf"], [n])
             for n, val in (("selc", 0.5), ("seld", 65536.0)):
                 V(80, lambda n=n: v.memset(T[n][:], 0.0), w=[n])
-                V(8, lambda n=n, val=val: v.tensor_scalar(T[n][:, 15:143:16], T.g8c[:], val, None, A.mult), ["g8c"], [n])
-            V(64, lambda: v.memset(T.kc8[:], 8.0), w=["kc8"])
+                V(8, lambda n=n, val=val: ts(T[n][:, 15:143:16], T.g8c[:], val, None, A.mult), ["g8c"], [n])
+            V(W / 2, lambda: v.memset(T.kc8[:], 8.0), w=["kc8"])
             for n, pat, base in (("krow", [[4096, 16], [0, NL]], 0), ("kkeep", [[0, NL], [256, 16]], -2048), ("kfill", [[0, NL], [256, 16]], 2048)):
-                op("g", 240, lambda n=n, pat=pat, base=base: g.iota(T[n][:], pat, base, 0, allow_small_or_imprecise_dtypes=True), w=[n])
-            for q in range(H):
-                V(136, lambda q=q: v.memset(B("x17", q)[:], 0.0), w=[("x17", q)])
-                V(72, lambda q=q: v.memset(B("mx", q)[:, 68:72], 0.0), w=[("mxpad", q)])
-                V(72, lambda q=q: v.memset(B("mn", q)[:, 68:72], 0.0), w=[("mnpad", q)])
-                V(72, lambda q=q: v.memset(B("a17", q)[:], 0), w=[("a17", q)])
-            for n, base, at, val in (("rk17", 0.0, (0,), BIG), ("mk17", 1.0, (0,), 0.0), ("rm17", 0.0, (15, 16), -1.0e6), ("rn17", 0.0, (15, 16), 1.0e6),
-                                     ("kw", 2128.0, (15,), -1968.0)):
-                V(68, lambda n=n, base=base: v.memset(T[n][:], base), w=[n])
+                op("g", 300, lambda n=n, pat=pat, base=base: g.iota(T[n][:], pat, base, 0, allow_small_or_imprecise_dtypes=True), w=[n])
+            for n, val in (("x17", 0.0), ("a17", 0), ("pb", 0)):
+                V(H * W17, lambda n=n, val=val: v.memset(T[n][:], val), w=[(n, q) for q in range(H)])
+            for n in ("mx", "mn"):
+                V(8, lambda n=n: v.memset(T[n][:, :, W17:W17 + 4], 0.0), w=[(n + "pad", q) for q in range(H)])
+            for n, base, at, val, m in (("rk17", 0.0, (0,), BIG, 17), ("mk17", 1.0, (0,), 0.0, 17), ("rm17", 0.0, (15, 16), -1.0e6, 17),
+                                        ("rn17", 0.0, (15, 16), 1.0e6, 17), ("tg17", 4096.0, (0,), -1.0e6, 17), ("kw", 2128.0, (15,), -1968.0, 17),
+                                        ("mk16", 1.0, (0,), 0.0, 16), ("rm16", 0.0, (15,), -1.0e6, 16)):
+                V(W17, lambda n=n, base=base: v.memset(T[n][:], base), w=[n])
                 for a in at:
-                    V(4, lambda n=n, a=a, val=val: v.memset(T[n][:, a::17], val), w=[n])
-            for n, base, at, val in (("mk16", 1.0, 0, 0.0), ("rm16", 0.0, 15, -1.0e6)):
-                V(64, lambda n=n, base=base: v.memset(T[n][:], base), w=[n])
-                V(4, lambda n=n, at=at, val=val: v.memset(T[n][:, at::16], val), w=[n])
-    for h in range(H):
-        V(64, lambda h=h: v.tensor_copy(T.m0[:, h, 64:128], T.nme[:, NL * h:NL * h + NL, :]), ["nme"], [("m0n", h)])
+                    V(NL, lambda n=n, a=a, val=val, m=m: v.memset(T[n][:, a::m], val), w=[n])
     nloc = [0]
 
-    def remote(dst, out, in_, sem, r):
+    def send(dst, land, out, in_, w, r):
         rid, pid = topo.addr(dst, core)
-        m = topo.mask(core, dst)
-        nloc[0] += len(topo.engines(core, dst))
-        op("g", 300, lambda: [(g.remote_dma(out, in_, T.sem[sem], T.sem.loc, pid, rid, m), None, 0)], r)
+        m, ne = topo.mask(core, dst), len(topo.engines(core, dst))
+        nloc[0] += ne
+        i = op("g", 300, lambda: [(g.remote_dma(out, in_, T.sem[land], T.sem.loc, pid, rid, m), None, 0)], r)
+        j = op("r", 0, None, (), w, sem=land, val=ne, lat=RLAT)
+        ops[j]["dep"].add(i)
 
-    def arrive(sem, w, sends):
-        ne = len(topo.engines(core, nxt))
-        i = op("r", 0, None, (), w, sem=sem, val=ne, lat=2500.0)
-        ops[i]["dep"].add(sends)
-
-    remote(opp, T.ls2[:], T.m0[:], "as2", [(("m0l", h), c) for h in range(H) for c in range(NL)] + [("m0n", h) for h in range(H)])
-    arrive("as2", ["ls2"], len(ops) - 1)
+    send(opp, "ls2", T.ls2[:], T.m0l[:], ["ls2"], [(("m0l", h), c) for h in range(H) for c in range(NL)])
+    send(opp, "lsn2", T.lsn2[:], T.nme[:], ["lsn2"], ["nme"])
 
     dn = [0]
+    pw = T.pw
     for t in range(1, R + 1):
         for h in range(H):
             b = lambda n: B(n, h)
             K = lambda *n: [(x, h) for x in n]
-            pu, pE = T["pu%d" % ((t * H + h) % 2)], T["pe%d" % ((t * H + h) % 2)]
-            ub, eb = "pu%d" % ((t * H + h) % 2), "pe%d" % ((t * H + h) % 2)
-            ck = T.pck[:, h, :, :, :]
+            eb = "pe%d" % ((t * H + h) % 2)
+            pE = T[eb]
+            ck = T.pck[:, h % CKS, :, :, 0:NL]
+            w0, w1 = pw[:, 2 * h, 0:W], pw[:, 2 * h + 1, 0:W]
+            k0, k1 = [("pw", 2 * h)], [("pw", 2 * h + 1)]
+            cs = slice(NL * h, NL * h + NL)
             if t == 1:
-                el, e15, ek = T.m0[:, h, 0:64], T.m0[:, h, 60:64], [(("m0l", h), c) for c in range(NL)]
-                sl, sk = b("l0")[:, 0:64], [(("l0", h), c) for c in range(NL)]
-                en3, enk = T.nme[:, NL * h:NL * h + NL, :], ["nme"]
-                zn, znk = T.nms[:, NL * h:NL * h + NL, :], ["nms"]
+                el, ek = T.m0l[:, h], [(("m0l", h), c) for c in range(NL)]
+                sl, sk = b("l0"), [(("l0", h), c) for c in range(NL)]
+                en, enk, zn, znk = T.nme[:, cs, :], ["nme"], T.nms[:, cs, :], ["nms"]
             else:
-                el, e15, ek = b("le%d" % t)[:, 0:64], b("le%d" % t)[:, 60:64], [("le%d" % t, h)]
-                en3, enk = b("le%d" % t)[:, 64:128], ek
+                el, ek, en, enk = b("le%d" % t), K("le%d" % t), b("len%d" % t), K("len%d" % t)
                 if t == 2:
-                    sl, sk, zs = T.ls2[:, h, 0:64], ["ls2"], T.ls2[:, h, 64:128]
+                    sl, sk, zn, znk = T.ls2[:, h], ["ls2"], T.lsn2[:, cs, :], ["lsn2"]
                 else:
-                    sl, sk, zs = b("ls3")[:, 0:64], K("ls3"), b("ls3")[:, 64:128]
-                zn, znk = b("zn")[:], K("zn")
-            gc = 80 + 1024 * 1.55
-            S(80 + 64 * 1.55, lambda y=b("v15"), l=e15: s.activation(y[:], T.ct[:].indirect(l), F.Copy), ["ct"] + ek, K("v15"))
-            for x, l, lk in (("y", sl, sk), ("v", el, ek)):
-                if (t, h, x) in ON_VECTOR:
-                    V(gc, lambda y=b(x), l=l: v.tensor_copy(y[:], T.ct[:].indirect(l)), ["ct"] + lk, K(x))
-                else:
-                    S(gc, lambda y=b(x), l=l: s.activation(y[:], T.ct[:].indirect(l), F.Copy), ["ct"] + lk, K(x))
-                if x == "y":
-                    ops[-1]["late"] = True
+                    sl, sk, zn, znk = b("ls3"), K("ls3"), b("lsn3"), K("lsn3")
+            def gather(n, l, lk, a, z):
+                for c in range(a, z, 64):
+                    e = min(c + 64, z)
+                    S(16 * (e - c) * 1.55, lambda c=c, e=e, y=b(n): act(y[:, 16 * (c - a):16 * (e - a)], T.ct[:].indirect(l[:, c:e]), F.Copy), ["ct"] + lk, [(n, h, c)])
+                return [(n, h, c) for c in range(a, z, 64)]
+            v15k = gather("v15", el, ek, W - NL, W)
+            yk = gather("y", sl, sk, 0, W)
+            for q in range(len(yk)): ops[-1 - q]["late"] = True
+            vk = gather("v", el, ek, 0, W)
 
             def vdiff(q, p, x):
-                m = te.matmul
-                m(p[:], T.ip[:], x[:, 512 * q:512 * q + 512], True, False)
-                if q == 0:
-                    return m(p[:], T.im[:], x[:, 64:576], False, True)
-                m(p[:, 0:448], T.im[:], x[:, 576:1024], False, False)
-                return m(p[:, 448:512], T.im[:], x[:, 0:64], False, True)
+                a = PC * q
+                mm(p[:, 0:PC], T.ip[:], x[:, a:a + PC], True, False)
+                if q < NP - 1:
+                    return mm(p[:, 0:PC], T.im[:], x[:, a + W:a + W + PC], False, True)
+                mm(p[:, 0:PC - W], T.im[:], x[:, a + W:NV], False, False)
+                return mm(p[:, PC - W:PC], T.im[:], x[:, 0:W], False, True)
 
             def ydiff(q, p, y, x):
-                te.matmul(p[:], T.ip[:], y[:, 512 * q:512 * q + 512], True, False)
-                for i in range(8):
-                    z = te.matmul(p[:, 64 * i:64 * i + 64], T.im[:], x[:], False, i == 7)
+                mm(p[:, 0:PC], T.ip[:], y[:, PC * q:PC * q + PC], True, False)
+                for i in range(RP):
+                    z = mm(p[:, W * i:W * i + W], T.im[:], x[:], False, i == RP - 1)
                 return z
 
             def sums(p, sel, x, con):
                 for m in range(16):
-                    te.matmul(p, sel[:, 15 - m:143 - m], x[:, m:1024:16], m == 0, False)
-                return te.matmul(p, T.ip[:], con[:], False, True)
+                    mm(p, sel[:, 15 - m:143 - m], x[:, m:NV:16], m == 0, False)
+                return mm(p, T.ip[:], con[:], False, True)
 
             for kind in (1, 0):
-                for q in range(2):
-                    pn = "pdiff%d" % (dn[0] % 2); dn[0] += 1
+                for q in range(NP):
+                    pn = "pd%d" % (dn[0] % NDIFF); dn[0] += 1
+                    a, z = PC * q, PC * q + PC
                     if kind == 0:
-                        P(1024, lambda q=q, p=T[pn], x=b("v"): vdiff(q, p, x), K("v") + ["ip", "im"], [pn], [pn])
-                        S(512, lambda q=q, p=T[pn], o=b("sg"): s.activation(o[:, 512 * q:512 * q + 512], p[:], F.Sign, bias=-0.5), [pn], [("sg%d" % q, h)], [pn])
+                        P(2 * PC, lambda q=q, p=T[pn], x=b("v"), f=vdiff: f(q, p, x), vk + ["ip", "im"], [pn], [pn])
+                        S(PC, lambda a=a, z=z, p=T[pn], o=b("sg"): act(o[:, a:z], p[:, 0:PC], F.Sign, bias=-0.5), [pn], [("sg", h, q)], [pn])
                     else:
-                        P(1024, lambda q=q, p=T[pn], y=b("y"), x=b("v15"): ydiff(q, p, y, x), K("v15", "y") + ["ip", "im"], [pn], [pn])
-                        S(512, lambda q=q, p=T[pn], o=b("ab"): s.activation(o[:, 512 * q:512 * q + 512], p[:], F.Abs), [pn], [("ab%d" % q, h)], [pn])
-            P(1088, lambda p=ck[:, 0, :, :], x=b("sg"): sums(p, T.selc, x, T.kc8), K("sg0", "sg1") + ["selc", "ip", "kc8"], K("pc"), ["pck"])
-            P(1088, lambda p=ck[:, 1, :, :], x=b("ab"): sums(p, T.seld, x, T.krow), K("ab0", "ab1") + ["seld", "ip", "krow"], K("pk"), ["pck"])
+                        P(2 * PC, lambda q=q, p=T[pn], y=b("y"), x=b("v15"), f=ydiff: f(q, p, y, x), v15k + yk + ["ip", "im"], [pn], [pn])
+                        S(PC, lambda a=a, z=z, p=T[pn], o=b("ab"): act(o[:, a:z], p[:, 0:PC], F.Abs), [pn], [("ab", h, q)], [pn])
+            P(17 * W, lambda p=ck[:, 1], x=b("ab"), f=sums: f(p, T.seld, x, T.krow), [("ab", h, q) for q in range(NP)] + ["seld", "ip", "krow"], K("pk"), ["pck"])
+            P(17 * W, lambda p=ck[:, 0], x=b("sg"), f=sums: f(p, T.selc, x, T.kc8), [("sg", h, q) for q in range(NP)] + ["selc", "ip", "kc8"], K("pc"), ["pck"])
             for c in range(NL):
-                S(64, lambda c=c, p=ck, x=b("x17"): s.activation(x[:, :, 17 * c:17 * c + 16], p[:, :, :, c], F.Copy), K("pc", "pk"), [("x17", h, c)], ["pck"])
+                S(32, lambda c=c, p=ck, x=b("x17"): act(x[:, :, 17 * c:17 * c + 16], p[:, :, :, c], F.Copy), K("pc", "pk"), [("x17", h, c)], ["pck"])
             x17k = [("x17", h)] + [("x17", h, c) for c in range(NL)]
-            V(64, lambda o=b("si"), x=en3: v.tensor_copy(o[:], x), enk, K("si"))
-            V(64, lambda o=b("s2"), x=b("si"): v.tensor_scalar(o[:, 0, :, :], x[:], 7, None, A.arith_shift_right), K("si"), K("s2h"))
-            V(64, lambda o=b("n2"), x=b("si"): v.tensor_scalar(o[:, 0, :], x[:], 127, None, A.bitwise_and), K("si"), K("n2h"))
-            V(128, lambda o=b("s2"), x=b("n2"): v.tensor_tensor(o[:, 1, :, :], x[:, 0, :], o[:, 0, :, :], A.add), K("n2h", "s2h"), K("s2l"))
+            V(W, lambda o=b("s2"), x=en: ts(o[:, 0, :, :], x[:], 7, None, A.arith_shift_right), enk, K("s2h"))
+            V(W, lambda o=b("sl"), x=en: ts(o[:], x[:], 127, None, A.bitwise_and), enk, K("sl"))
+            V(2 * W, lambda o=b("s2"), x=b("sl"): tt(o[:, 1, :, :], x[:], o[:, 0, :, :], A.add), K("sl", "s2h"), K("s2l"))
+            V(W17, lambda x=b("x17"), o=b("cc"): scan(o[:], T.mk17[:], x[:, 0, :], 0.0, A.mult, A.add), x17k + ["mk17"], K("cc"))
+            V(W17, lambda x=b("x17"), o=b("km"): scan(o[:], T.rk17[:], x[:, 1, :], 0.0, A.add, A.min), x17k + ["rk17"], K("km"))
+            V(W17, lambda x=b("cc"), o=b("par"): ts(o[:], x[:], 1, None, A.bitwise_and), K("cc"), K("par"))
+            V(NL, lambda x=b("km"), o=b("pb"): ts(o[:, 0::17], x[:, 15::17], 4096, None, A.bitwise_and), K("km"), K("pb"))
+            V(W17, lambda x=b("par"), o=b("st"): ts(o[:], x[:], -8192.0, 4096.0, A.mult, A.add), K("par"), K("st"))
+            V(W17, lambda x=b("pb"), o=b("od"): scan(o[:], T.tg17[:], x[:], 0.0, A.subtract, A.max), K("pb") + ["tg17"], K("od"))
+            V(NL, lambda x=b("km"), o=b("st"): ts(o[:, 0::17], x[:, 15::17], 61440, None, A.bitwise_and), K("km"), K("st"))
+            V(W17, lambda x=b("st"), o=b("pos"): scan(o[:], T.mk17[:], x[:], 0.0, A.mult, A.add), K("st") + ["mk17"], K("pos"))
+            V(W17, lambda x=b("pos"), o=b("mx"): scan(o[:, W17 - 1::-1], T.rm17[:, ::-1], x[:, ::-1], 0.0, A.add, A.max), K("pos") + ["rm17"], K("mx"))
+            V(W17, lambda x=b("pos"), o=b("mn"): scan(o[:, W17 - 1::-1], T.rn17[:, ::-1], x[:, ::-1], 0.0, A.add, A.min), K("pos") + ["rn17"], K("mn"))
+            S(W17, lambda x=b("pos"), o=b("g1"): act(o[:], x[:], F.Sign, bias=63488.0, scale=-1.0), K("pos"), K("g1"))
+            S(W17, lambda x=b("pos"), o=b("g2"): act(o[:], x[:], F.Sign, bias=-2048.0, scale=-1.0), K("pos"), K("g2"))
+            S(W17, lambda x=b("x17"), o=b("w"): act(o[:], x[:, 0, :], F.Sign, bias=-9.5), x17k, K("w"))
             if t > 1:
-                V(64, lambda o=b("zn"), x=zs: v.tensor_copy(o[:], x), sk, K("zn"))
-            V(68, lambda x=b("x17"), o=b("cc"): v.tensor_tensor_scan(o[:], T.mk17[:], x[:, 0, :], 0.0, A.mult, A.add), x17k + ["mk17"], K("cc"))
-            V(68, lambda x=b("x17"), o=b("km"): v.tensor_tensor_scan(o[:], T.rk17[:], x[:, 1, :], 0.0, A.add, A.min), x17k + ["rk17"], K("km"))
-            V(68, lambda x=b("cc"), o=b("par"): v.tensor_scalar(o[:], x[:], 1, None, A.bitwise_and), K("cc"), K("par"))
-            V(68, lambda x=b("par"), o=b("st"): v.tensor_scalar(o[:], x[:], -8192.0, 4096.0, A.mult, A.add), K("par"), K("st"))
-            V(4, lambda x=b("km"), o=b("st"): v.tensor_scalar(o[:, 0::17], x[:, 15::17], 61440, None, A.bitwise_and), K("km"), K("st"))
-            V(68, lambda x=b("st"), o=b("pos"): v.tensor_tensor_scan(o[:], T.mk17[:], x[:], 0.0, A.mult, A.add), K("st") + ["mk17"], K("pos"))
-            V(68, lambda x=b("pos"), o=b("mx"): v.tensor_tensor_scan(o[:, 67::-1], T.rm17[:, ::-1], x[:, ::-1], 0.0, A.add, A.max), K("pos") + ["rm17"], K("mx"))
-            V(68, lambda x=b("pos"), o=b("mn"): v.tensor_tensor_scan(o[:, 67::-1], T.rn17[:, ::-1], x[:, ::-1], 0.0, A.add, A.min), K("pos") + ["rn17"], K("mn"))
-            S(68, lambda x=b("pos"), o=b("g1"): s.activation(o[:], x[:], F.Sign, bias=63488.0, scale=-1.0), K("pos"), K("g1"))
-            S(68, lambda x=b("pos"), o=b("g2"): s.activation(o[:], x[:], F.Sign, bias=-2048.0, scale=-1.0), K("pos"), K("g2"))
-            S(68, lambda x=b("x17"), o=b("w"): s.activation(o[:], x[:, 0, :], F.Sign, bias=-9.5), x17k, K("w"))
-            if t > 1:
-                V(136, lambda x=b("x17"), o=b("d1"), a=b("a17"): v.tensor_tensor(o[:], x[:, 0, :], a[:], A.subtract), x17k + K("a17"), K("d1"))
+                V(2 * W17, lambda x=b("x17"), o=b("d1"), a=b("a17"): tt(o[:], x[:, 0, :], a[:], A.subtract), x17k + K("a17"), K("d1"))
             dk, dx = (K("d1"), b("d1")) if t > 1 else (x17k, b("x17")[:, 0, :])
-            S(68, lambda x=dx, o=b("u"): s.activation(o[:], x[:], F.Sign, bias=5.5, scale=-1.0), dk, K("u"))
+            S(W17, lambda x=dx, o=b("u"): act(o[:], x[:], F.Sign, bias=5.5, scale=-1.0), dk, K("u"))
 
             def usum(p, h):
-                o = p[:, 0, :, 0:17]
-                te.matmul(o, T.ip[:], T.kw[:], True, False)
-                te.matmul(o, T.i16[:], B("w", h)[:], False, False)
-                te.matmul(o, T.i32[:], B("u", h)[:], False, False)
-                te.matmul(o, T.i16th[:], B("pos", h)[:], False, False)
-                te.matmul(o, T.i2048[:], B("g1", h)[:], False, False)
-                te.matmul(o, T.i2048[:], B("g2", h)[:], False, False)
-                te.matmul(o, T.im[:], B("mx", h)[:, 0:68], False, False)
-                te.matmul(o, T.ip[:], B("mx", h)[:, 1:69], False, False)
-                te.matmul(o, T.ip[:], B("mn", h)[:, 0:68], False, False)
-                return te.matmul(o, T.im[:], B("mn", h)[:, 1:69], False, True)
-            P(680, lambda p=pu, h=h: usum(p, h), K("pos", "g1", "g2", "u", "w", "mx", "mn", "mxpad", "mnpad") + ["ip", "im", "i16th", "i16", "i32", "i2048", "kw"], ["U" + ub], [ub])
+                o = p[:, 0:NL, 32:49]
+                mm(o, T.ip[:], T.kw[:], True, False)
+                for n, c in (("od", "i4"), ("w", "i16"), ("u", "i32"), ("pos", "i16th"), ("g1", "i2048"), ("g2", "i2048")):
+                    mm(o, T[c][:], B(n, h)[:], False, False)
+                mm(o, T.im[:], B("mx", h)[:, 0:W17], False, False)
+                mm(o, T.ip[:], B("mx", h)[:, 1:W17 + 1], False, False)
+                mm(o, T.ip[:], B("mn", h)[:, 0:W17], False, False)
+                return mm(o, T.im[:], B("mn", h)[:, 1:W17 + 1], False, True)
+            P(11 * W17, lambda p=pE, h=h: usum(p, h), K("od", "pos", "g1", "g2", "u", "w", "mx", "mn", "mxpad", "mnpad") + ["ip", "im", "i16th", "i16", "i4", "i32", "i2048", "kw"], ["U" + eb], [eb])
             for a, sk2 in ((0, "s2h"), (1, "s2l")):
-                V(64, lambda a=a, o=b("q1"), x=b("s2"), p=pu: v.tensor_tensor(o[:, a, :, :], x[:, a, :, :], p[:, 0, :, 0:16], A.add), K(sk2) + ["U" + ub], K("q1%d" % a), [ub])
-            for p_ in range(16):
-                V(64, lambda p_=p_, o=b("o1"), x=b("q1"): v.tensor_scalar(o[:, :, :, p_, :], x[:], 256.0 * p_ - 2048.0, 256.0 * p_ - 1792.0, A.max, A.min), K("q10", "q11"), [("o1", h, p_)])
+                V(W, lambda a=a, o=b("q1"), x=b("s2"), p=pE: tt(o[:, a, :, :], x[:, a, :, :], p[:, 0:NL, 32:48], A.add), K(sk2) + ["U" + eb], K("q1%d" % a), [eb])
+            V(2 * W, lambda o=b("qx"), x=b("q1"): tt(o[:], x[:, :, :, 0::2], x[:, :, :, 1::2], A.max), K("q10", "q11"), K("qx"))
+            V(2 * W, lambda o=b("qp"), x=b("q1"): tt(o[:, :, :, 0, :], x[:, :, :, 0::2], x[:, :, :, 1::2], A.min), K("q10", "q11"), K("qpe"))
+            V(W, lambda o=b("qp"), x=b("qx"): ts(o[:, :, :, 1, :], x[:], -16640.0, None, A.add), K("qx"), K("qpo"))
+            for p_ in range(8):
+                V(W, lambda p_=p_, o=b("o1"), x=b("qp"): ts(o[:, :, :, p_, :, :], x[:], 512.0 * p_ - 2048.0, 512.0 * p_ - 1792.0, A.max, A.min), K("qpe", "qpo"), [("o1", h, p_)])
 
             def picked(p, q, o, n, f):
                 for k in range(n):
-                    z = te.matmul(p[:, q:q + 2, :, 8 * f:8 * f + 8], T.iph[:], o[:, :, :, 8 * f:8 * f + 8, k], k == 0, k == n - 1)
+                    for a, c in ((0, T.i127h), (1, T.iph)):
+                        x = o[:, a, :, 8 * f:8 * f + 8, k] if n == 17 else o[:, a, :, 4 * f:4 * f + 4, :, k]
+                        z = mm(p[:, 0:NL, q + 8 * f:q + 8 * f + 8], c[:], x, k == 0 and a == 0, k == n - 1 and a == 1)
                 return z
             for f in range(2):
-                P(1024, lambda p=pE, o=b("o1"), f=f: picked(p, 0, o, 16, f), [("o1", h, p_) for p_ in range(8 * f, 8 * f + 8)] + ["iph"], ["E%d" % f + eb], [eb])
-            V(64, lambda o=b("eh"), p=pE: v.tensor_scalar(o[:], p[:, 0, :, :], 127.0, None, A.mult), ["E0" + eb, "E1" + eb], K("eh"), [eb])
-            V(64, lambda o=b("ei"), x=b("eh"), p=pE: v.tensor_tensor(o[:], x[:], p[:, 1, :, :], A.add), ["E0" + eb, "E1" + eb] + K("eh"), K("ei"), [eb])
-            V(64, lambda o=b("xx"), x=b("ei"): v.tensor_scalar(o[:], x[:], 16383, None, A.bitwise_and), K("ei"), K("xx"))
-            pw = T.pw
-            c0 = 2 * h
-            V(64, lambda x=b("xx"), o=b("dl"): v.tensor_scalar(o[:], x[:], 12288.0, None, A.is_ge), K("xx"), K("dl"))
-            V(64, lambda x=b("dl"), o=b("ii"): v.tensor_tensor_scan(o[:], T.mk16[:], x[:], 0.0, A.mult, A.add), K("dl") + ["mk16"], K("ii"))
-            V(64, lambda x=b("ii"), o=b("nb"): v.tensor_tensor_scan(o[:, ::-1], T.rm16[:, ::-1], x[:, ::-1], 0.0, A.add, A.max), K("ii") + ["rm16"], K("nb"))
+                P(16 * max(64, W // 2), lambda p=pE, o=b("o1"), f=f, pk=picked: pk(p, 0, o, 8, f), [("o1", h, p_) for p_ in range(4 * f, 4 * f + 4)] + ["iph", "i127h"], ["E%d" % f + eb], [eb])
+            V(W, lambda o=b("ei"), p=pE: v.tensor_copy(o[:], p[:, 0:NL, 0:16]), ["E0" + eb, "E1" + eb], K("ei"), [eb])
+            V(W, lambda o=b("xx"), x=b("ei"): ts(o[:], x[:], 16383, None, A.bitwise_and), K("ei"), K("xx"))
+            V(W, lambda x=b("xx"), o=b("dl"): ts(o[:], x[:], 12288.0, None, A.is_ge), K("xx"), K("dl"))
+            V(W, lambda x=b("dl"), o=b("ii"): scan(o[:], T.mk16[:], x[:], 0.0, A.mult, A.add), K("dl") + ["mk16"], K("ii"))
+            V(W, lambda x=b("ii"), o=b("nb"): scan(o[:, ::-1], T.rm16[:, ::-1], x[:, ::-1], 0.0, A.add, A.max), K("ii") + ["rm16"], K("nb"))
 
             def tsum(p, h):
-                o = p[:, 0, :, 20:36]
-                te.matmul(o, T.ip[:], T.kkeep[:], True, False)
-                te.matmul(o, T.i8192[:], B("dl", h)[:], False, False)
-                te.matmul(o, T.im256[:], B("ii", h)[:], False, True)
-                o = p[:, 0, :, 36:52]
-                te.matmul(o, T.ip[:], T.kfill[:], True, False)
-                return te.matmul(o, T.im256[:], B("nb", h)[:], False, True)
-            P(320, lambda p=pu, h=h: tsum(p, h), K("dl", "ii", "nb") + ["i8192", "im256", "ip", "kkeep", "kfill"], ["T" + ub], [ub])
-            V(64, lambda x=b("xx"), c0=c0: v.tensor_scalar(pw[:, c0, :], x[:], -8192.0, 0.0, A.add, A.max), K("xx"), [("pw", c0)])
-            V(64, lambda x=b("xx"), o=b("n32"): v.tensor_scalar(o[:], x[:], 4096.0, 32.0, A.is_lt, A.mult), K("xx"), K("n32"))
-            V(64, lambda x=b("xx"), c0=c0, t=t: v.tensor_scalar(pw[:, c0 + 1, :], x[:], 8192.0, 77.0 * t, A.is_ge, A.mult), K("xx"), [("pw", c0 + 1)])
-            V(64, lambda x=b("xx"), c0=c0: v.tensor_tensor(pw[:, c0 + 1, :], x[:], pw[:, c0 + 1, :], A.add), K("xx"), [("pw", c0 + 1)])
-            V(64, lambda x=b("n32"), c0=c0: v.tensor_tensor(pw[:, c0, :], x[:], pw[:, c0, :], A.add), K("n32"), [("pw", c0)])
-            V(64, lambda x=zn, o=b("az"), c0=c0: v.tensor_tensor(o[:], x, pw[:, c0, :], A.mult), znk + [("pw", c0)], K("az"))
-            V(64, lambda x=b("az"), o=b("sf"): v.tensor_scalar(o[:], x[:], 5, 4095, A.arith_shift_right, A.bitwise_and), K("az"), K("sf"))
-            V(64, lambda x=b("sf"), o=b("b2"), c0=c0: v.tensor_tensor(o[:], x[:], pw[:, c0 + 1, :], A.add), K("sf") + [("pw", c0 + 1)], K("b2"))
-            V(64, lambda x=b("b2"), o=b("n2"): v.tensor_scalar(o[:, 0, :], x[:], 7, 31, A.arith_shift_right, A.bitwise_and), K("b2"), K("n2h"))
-            V(64, lambda x=b("b2"), o=b("n2"): v.tensor_scalar(o[:, 1, :], x[:], 127, None, A.bitwise_and), K("b2"), K("n2l"))
+                o = p[:, 0:NL, 32:48]
+                mm(o, T.ip[:], T.kkeep[:], True, False)
+                mm(o, T.i8192[:], B("dl", h)[:], False, False)
+                mm(o, T.im256[:], B("ii", h)[:], False, True)
+                o = p[:, 0:NL, 0:16]
+                mm(o, T.ip[:], T.kfill[:], True, False)
+                return mm(o, T.im256[:], B("nb", h)[:], False, True)
+            P(5 * W, lambda p=pE, h=h: tsum(p, h), K("dl", "ii", "nb") + ["i8192", "im256", "ip", "kkeep", "kfill"], ["T" + eb, "U" + eb, "E0" + eb, "E1" + eb], [eb])
+            V(W, lambda x=b("xx"), o=w0: ts(o, x[:], -8192.0, 0.0, A.add, A.max), K("xx"), k0)
+            V(W, lambda x=b("xx"), o=b("n32"): ts(o[:], x[:], 4096.0, 32.0, A.is_lt, A.mult), K("xx"), K("n32"))
+            V(W, lambda x=b("xx"), o=w1, t=t: ts(o, x[:], 8192.0, 77.0 * t, A.is_ge, A.mult), K("xx"), k1)
+            V(W, lambda x=b("n32"), o=w0: tt(o, x[:], o, A.add), K("n32"), k0)
+            V(W, lambda x=b("xx"), o=w1: tt(o, x[:], o, A.add), K("xx"), k1)
+            V(W, lambda x=zn, o=b("az"), y=w0: tt(o[:], x, y, A.mult), znk + k0, K("az"))
+            V(W, lambda x=b("az"), o=b("sf"): ts(o[:], x[:], 5, 4095, A.arith_shift_right, A.bitwise_and), K("az"), K("sf"))
+            V(W, lambda x=b("sf"), o=b("b2"), y=w1: tt(o[:], x[:], y, A.add), K("sf") + k1, K("b2"))
+            V(W, lambda x=b("b2"), o=b("n2"): ts(o[:, 0, :], x[:], 7, 31, A.arith_shift_right, A.bitwise_and), K("b2"), K("n2h"))
+            V(W, lambda x=b("b2"), o=b("n2"): ts(o[:, 1, :], x[:], 127, None, A.bitwise_and), K("b2"), K("n2l"))
             for a, sk2 in ((0, "s2h"), (1, "s2l")):
-                V(64, lambda a=a, o=b("q2"), x=b("s2"), p=pu: v.tensor_tensor(o[:, a, :, 16:32], x[:, a, :, :], p[:, 0, :, 36:52], A.add), K(sk2) + ["T" + ub], K("q2b%d" % a), [ub])
-            V(64, lambda x=b("n2"), p=pu, c0=c0: v.tensor_tensor(pw[:, c0, :], x[:, 0, :], p[:, 0, :, 20:36], A.add), K("n2h") + ["T" + ub], [("pw", c0)], [ub])
-            V(64, lambda x=b("n2"), o=b("q2"), c0=c0: v.tensor_tensor(o[:, 1, :, 0:16], x[:, 1, :], pw[:, c0, :], A.add), K("n2l") + [("pw", c0)], K("q2a1"))
-            V(64, lambda o=b("q2"), c0=c0: v.tensor_copy(o[:, 0, :, 0:16], pw[:, c0, :]), [("pw", c0)], K("q2a0"))
+                V(W, lambda a=a, o=b("q2"), x=b("s2"), p=pE: tt(o[:, a, :, 16:32], x[:, a, :, :], p[:, 0:NL, 0:16], A.add), K(sk2) + ["T" + eb], K("q2b%d" % a), [eb])
+            V(W, lambda x=b("n2"), p=pE, o=w0: tt(o, x[:, 0, :], p[:, 0:NL, 32:48], A.add), K("n2h") + ["T" + eb], k0, [eb])
+            V(W, lambda x=b("n2"), o=b("q2"), y=w0: tt(o[:, 1, :, 0:16], x[:, 1, :], y, A.add), K("n2l") + k0, K("q2a1"))
+            V(W, lambda o=b("q2"), y=w0: v.tensor_copy(o[:, 0, :, 0:16], y), k0, K("q2a0"))
             for i in range(16):
-                V(68, lambda i=i, o=b("o2"), x=b("q2"): v.tensor_scalar(o[:, :, :, i, :], x[:, :, :, i:i + 17], 256.0 * i - 2048.0, 256.0 * i - 1792.0, A.max, A.min), K("q2a0", "q2a1", "q2b0", "q2b1"), [("o2", h, i)])
+                V(W17, lambda i=i, o=b("o2"), x=b("q2"): ts(o[:, :, :, i, :], x[:, :, :, i:i + 17], 256.0 * i - 2048.0, 256.0 * i - 1792.0, A.max, A.min), K("q2a0", "q2a1", "q2b0", "q2b1"), [("o2", h, i)])
             for f in range(2):
-                P(1088, lambda p=pE, o=b("o2"), f=f: picked(p, 2, o, 17, f), [("o2", h, i) for i in range(8 * f, 8 * f + 8)] + ["iph"], ["R%d" % f + eb], [eb])
-            V(64, lambda o=b("fh"), p=pE: v.tensor_scalar(o[:], p[:, 2, :, :], 127.0, None, A.mult), ["R0" + eb, "R1" + eb], K("fh"), [eb])
-            V(64, lambda o=b("fi"), x=b("fh"), p=pE: v.tensor_tensor(o[:], x[:], p[:, 3, :, :], A.add), ["R0" + eb, "R1" + eb] + K("fh"), K("fi"), [eb])
-            V(64, lambda o=b("nm"), x=b("fi"): v.tensor_scalar(o[:], x[:], 4095, None, A.bitwise_and), K("fi"), K("nm"))
+                P(34 * max(64, W // 2), lambda p=pE, o=b("o2"), f=f, pk=picked: pk(p, 16, o, 17, f), [("o2", h, i) for i in range(8 * f, 8 * f + 8)] + ["iph", "i127h"], ["R%d" % f + eb], [eb])
+            nm, nmk = b("nm%d" % t), K("nm%d" % t)
+            V(W, lambda o=b("fi"), p=pE: v.tensor_copy(o[:], p[:, 0:NL, 16:32]), ["R0" + eb, "R1" + eb], K("fi"), [eb])
+            V(W, lambda o=nm, x=b("fi"): ts(o[:], x[:], 4095, None, A.bitwise_and), K("fi"), nmk)
             if t < R:
-                m = b("m%d" % t)
-                lists(m[:, 0:64], b("nm"), K("nm"), ("m%dl" % t, h))
-                V(64, lambda m=m, x=b("nm"): v.tensor_copy(m[:, 64:128], x[:]), K("nm"), [("m%dn" % t, h)])
-                mk = [(("m%dl" % t, h), c) for c in range(NL)] + [("m%dn" % t, h)]
-                remote(nxt, b("le%d" % (t + 1))[:], m[:], "ae%d%d" % (t + 1, h), mk)
-                arrive("ae%d%d" % (t + 1, h), K("le%d" % (t + 1)), len(ops) - 1)
+                n = t + 1
+                lists(b("ml%d" % t), nm, nmk, ("ml%d" % t, h))
+                mk = [(("ml%d" % t, h), c) for c in range(NL)]
+                send(nxt, "le%d%d" % (n, h), b("le%d" % n)[:], b("ml%d" % t)[:], K("le%d" % n), mk)
+                send(nxt, "len%d%d" % (n, h), b("len%d" % n)[:], nm[:], K("len%d" % n), nmk)
                 if t + 2 <= R:
-                    remote(prv, b("ls%d" % (t + 2))[:], m[:], "as%d%d" % (t + 2, h), mk)
-                    arrive("as%d%d" % (t + 2, h), K("ls%d" % (t + 2)), len(ops) - 1)
-                V(64, lambda x=b("nb"), o=b("ni"): v.tensor_copy(o[:], x[:]), K("nb"), K("ni"))
-                V(64, lambda x=b("ni"), o=b("a17"): v.tensor_scalar(o[:, :, 0:16], x[:], 1, None, A.bitwise_and), K("ni"), K("a17"))
+                    send(prv, "ls3%d" % h, b("ls3")[:], b("ml%d" % t)[:], K("ls3"), mk)
+                    send(prv, "lsn3%d" % h, b("lsn3")[:], nm[:], K("lsn3"), nmk)
+                V(W, lambda x=b("nb"), o=b("ni"): v.tensor_copy(o[:], x[:]), K("nb"), K("ni"))
+                V(W, lambda x=b("ni"), o=b("a17"): ts(o[:, :, 0:16], x[:], 1, None, A.bitwise_and), K("ni"), K("a17"))
             if t >= R - 1:
-                V(64, lambda x=b("nm"), o=b("tm"): v.tensor_scalar(o[:, :, 0, :], x[:], T.meven[:], None, A.mult), K("nm") + ["meven"], K("tm0"))
-                V(64, lambda x=b("nm"), o=b("tm"): v.tensor_scalar(o[:, :, 1, :], x[:], T.modd[:], None, A.mult), K("nm") + ["modd"], K("tm1"))
-                V(128, lambda x=b("tm"), o=b("tt"): v.transpose(o[:], x[:]), K("tm0", "tm1"), K("tt"))
-                V(128, lambda x=b("tt"), o=b("yo%d" % t): v.tensor_tensor(o[:], x[:, :, 0, :], x[:, :, 1, :], A.add), K("tt"), K("yo%d" % t))
-                remote(nxt if t == R else prv, b("ly%d" % t)[:], b("yo%d" % t)[:], "ay%d%d" % (t, h), K("yo%d" % t))
-                arrive("ay%d%d" % (t, h), K("ly%d" % t), len(ops) - 1)
+                V(W, lambda x=nm, o=b("tm"): ts(o[:, :, 0, :], x[:], T.meven[:], None, A.mult), nmk + ["meven"], K("tm0"))
+                V(W, lambda x=nm, o=b("tm"): ts(o[:, :, 1, :], x[:], T.modd[:], None, A.mult), nmk + ["modd"], K("tm1"))
+                V(2 * W, lambda x=b("tm"), o=b("tt"): v.transpose(o[:], x[:]), K("tm0", "tm1"), K("tt"))
+                V(2 * W, lambda x=b("tt"), o=b("yo%d" % t): tt(o[:], x[:, :, 0, :], x[:, :, 1, :], A.add), K("tt"), K("yo%d" % t))
+                send(nxt if t == R else prv, "ly%d%d" % (t, h), b("ly%d" % t)[:], b("yo%d" % t)[:], K("ly%d" % t), K("yo%d" % t))
                 y = T.yenz if t == R else T.ysub
-                op("y", 60, lambda y=y, x=b("ly%d" % t), h=h: [(g.sync.dma_start(y[:, 64 * h:64 * h + 64], x[:]), "out", 16)], K("ly%d" % t))
+                op("y", 60, lambda y=y, x=b("ly%d" % t), h=h: [(g.sync.dma_start(y[:, W * h:W * h + W], x[:]), "out", 16)], K("ly%d" % t))
 
-    WAKE = 60.0
     n = len(ops)
     succ = [[] for i in range(n)]
     for i, o in enumerate(ops):
         for d in o["dep"]: succ[d].append(i)
         o["pr"] = i + (LATE if o.get("late") else 0)
-    rank_of_op = sorted(range(n), key=lambda i: ops[i]["pr"])
+    by_pr = sorted(range(n), key=lambda i: ops[i]["pr"])
 
     def schedule(known):
         left = [len(o["dep"]) for o in ops]
         ready = [0.0] * n
-        free, order, cand = {}, [], {}
-        urgent = {}
+        free, order, cand, urgent, out = {}, [], {}, {}, set()
         if known:
-            for i in rank_of_op: urgent.setdefault(ops[i]["eng"], []).append(i)
-        out = set()
+            for i in by_pr: urgent.setdefault(ops[i]["eng"], []).append(i)
         end = 0.0
         for i in range(n):
             if not left[i]: cand.setdefault(ops[i]["eng"], []).append(i)
@@ -385,15 +378,13 @@ def rank_program(g, core, T, topo):
                     starts.append((st, i))
                 lo = min(starts)[0]
                 pr, st, i = min((ops[i]["pr"], st, i) for st, i in starts if st <= lo + 20.0)
-                key = (st, i)
-                if best is None or key < best[0]: best = (key, e, i)
+                if best is None or (st, i) < best[0]: best = ((st, i), e, i)
             if best is None: break
             (st, _), e, i = best
             cand[e].remove(i)
             out.add(i)
-            o = ops[i]
-            free[e] = st + o["cost"]
-            fin = st + o["cost"] + o["lat"]
+            free[e] = st + ops[i]["cost"]
+            fin = free[e] + ops[i]["lat"]
             end = max(end, fin)
             order.append(i)
             for j in succ[i]:
@@ -406,11 +397,9 @@ def rank_program(g, core, T, topo):
     for k in range(PASSES):
         end, order, known = schedule(known)
         if best is None or end < best[0]: best = (end, order)
-    order = best[1]
 
-    count, done, waited = {}, {}, {}
-    ndma = [0]
-    for i in order:
+    count, done, waited, ndma = {}, {}, {}, 0
+    for i in best[1]:
         o = ops[i]
         e = o["eng"]
         if e == "r":
@@ -429,15 +418,14 @@ def rank_program(g, core, T, topo):
             ins, sm, inc = x[0]
             if sm is not None:
                 ins.then_inc(T.sem[sm], inc)
-                if sm == "out": ndma[0] += inc
-            done[i] = (sm, o["val"])
-            if sm is None: done[i] = ("loc", 0)
+                if sm == "out": ndma += inc
+            done[i] = (sm, o["val"]) if sm else ("loc", 0)
         else:
             sm = engsem[e]
             x.then_inc(T.sem[sm], 1)
             count[sm] = count.get(sm, 0) + 1
             done[i] = (sm, count[sm])
-    g.sync.wait_ge(T.sem.out, ndma[0])
+    g.sync.wait_ge(T.sem.out, ndma)
     g.wait_ge(T.sem.loc, nloc[0])
     for sm in count:
         g.wait_ge(T.sem[sm], count[sm])

from concourse.bass import DstId, RemoteDMATransfer
from concourse.mybir import dt, AluOpType as A, ActivationFunctionType as F

H = 2
NL = 12 // H
W, W17 = 16 * NL, 17 * NL
NV = 16 * W
RP = 8 if NL <= 4 else 4
NP, PC = 16 // RP, RP * W
R = 3
CY, VO, SO, PCY = 0.83, 50.0, 65.0, 0.42
LATE, HOLD, AHEAD, PASSES, WAKE, RLAT = 100, 400.0, 0.8, 4, 60.0, 2500.0
BIG = 1.0e9
CKS = 4 if NL <= 4 else 2
NDIFF = 4

IDENT = (("ip", 1.0, "bfloat16"), ("im", -1.0, "bfloat16"), ("i16th", 1.0 / 16, "bfloat16"), ("i2048", 2048.0, "bfloat16"),
         ("i16", 16.0, "bfloat16"), ("i32", 32.0, "bfloat16"), ("i4", 4.0, "bfloat16"), ("i8192", 8192.0, "bfloat16"),
         ("im256", -256.0, "bfloat16"), ("iph", 1.0, "float16"), ("i127h", 127.0, "float16"))
SCRATCH = {
    "ct": ("sbuf", [128, 4096], "bfloat16"),
    "en": ("sbuf", [128, 192], "int32"), "su": ("sbuf", [128, 192], "int32"),
    "one": ("sbuf", [128, 128], "float32"), "idf": ("sbuf", [128, 128], "float32"),
    "g8a": ("sbuf", [128, 8], "float32"), "g8b": ("sbuf", [128, 8], "float32"), "g8c": ("sbuf", [128, 8], "float32"),
    "pid": ("sbuf", [128, 1], "int32"), "pbit": ("sbuf", [128, 1], "int32"),
    "modd": ("sbuf", [128, 1], "float32"), "meven": ("sbuf", [128, 1], "float32"),
    "selc": ("sbuf", [128, 160], "bfloat16"), "seld": ("sbuf", [128, 160], "bfloat16"),
    "kc8": ("sbuf", [128, W], "bfloat16"), "krow": ("sbuf", [128, W], "bfloat16"),
    "kw": ("sbuf", [128, W17], "bfloat16"), "tg17": ("sbuf", [128, W17], "float32"),
    "kkeep": ("sbuf", [128, W], "bfloat16"), "kfill": ("sbuf", [128, W], "bfloat16"),
    "mk17": ("sbuf", [128, W17], "float32"), "rk17": ("sbuf", [128, W17], "float32"),
    "rm17": ("sbuf", [128, W17], "float32"), "rn17": ("sbuf", [128, W17], "float32"),
    "mk16": ("sbuf", [128, W], "float32"), "rm16": ("sbuf", [128, W], "float32"),
    "m0l": ("sbuf", [128, H, W], "uint16"), "ls2": ("sbuf", [128, H, W], "uint16"), "lsn2": ("sbuf", [128, 12, 16], "int32"),
    "nme": ("sbuf", [128, 12, 16], "int32"), "nms": ("sbuf", [128, 12, 16], "int32"),
    "pck": ("psum", [128, CKS, 2, 16, 16 // CKS], "float32"),
    "pe0": ("psum", [128, 8, 64], "float32"), "pe1": ("psum", [128, 8, 64], "float32"),
    "pw": ("psum", [128, 2 * CKS, 256 // CKS], "float32"),
}
for _q in range(NDIFF):
    SCRATCH["pd%d" % _q] = ("psum", [128, 512], "float32")
for _n, _v, _d in IDENT:
    SCRATCH[_n] = ("sbuf", [128, 128], _d)
for _k in ("e", "s"):
    SCRATCH["xm" + _k] = ("sbuf", [128, 12, 2, 16], "float32")
    SCRATCH["xt" + _k] = ("sbuf", [128, 12, 2, 16], "float32")
for _n, _s, _d in (
        ("v", [NV], "bfloat16"), ("y", [NV], "bfloat16"), ("sg", [NV], "bfloat16"), ("ab", [NV], "bfloat16"), ("v15", [W], "bfloat16"),
        ("x17", [2, W17], "float32"), ("km", [W17], "int32"), ("cc", [W17], "int32"), ("par", [W17], "int32"),
        ("st", [W17], "int32"), ("pb", [W17], "int32"), ("od", [W17], "bfloat16"), ("pos", [W17], "bfloat16"),
        ("g1", [W17], "bfloat16"), ("g2", [W17], "bfloat16"), ("mx", [W17 + 4], "bfloat16"), ("mn", [W17 + 4], "bfloat16"),
        ("a17", [NL, 17], "int32"), ("d1", [W17], "float32"), ("u", [W17], "bfloat16"), ("w", [W17], "bfloat16"),
        ("s2", [2, NL, 16], "int32"), ("q1", [2, NL, 16], "float32"), ("qx", [2, NL, 8], "float32"), ("qp", [2, NL, 2, 8], "float16"),
        ("o1", [2, NL, 8, 2, 8], "float16"), ("ei", [W], "int32"), ("xx", [W], "int32"), ("n32", [W], "float32"),
        ("az", [W], "int32"), ("sf", [W], "int32"), ("b2", [W], "int32"), ("n2", [2, W], "int32"), ("sl", [W], "int32"),
        ("dl", [W], "bfloat16"), ("ii", [W], "bfloat16"), ("nb", [W], "bfloat16"), ("ni", [W], "int32"),
        ("q2", [2, NL, 32], "float16"), ("o2", [2, NL, 16, 17], "float16"), ("fi", [W], "int32"),
        ("nm1", [NL, 16], "int32"), ("nm2", [NL, 16], "int32"), ("nm3", [NL, 16], "int32"),
        ("tm", [NL, 2, 16], "float32"), ("tt", [NL, 2, 16], "float32"), ("l0", [W], "uint16"),
        ("ml1", [W], "uint16"), ("ml2", [W], "uint16"), ("le2", [W], "uint16"), ("le3", [W], "uint16"), ("ls3", [W], "uint16"),
        ("len2", [NL, 16], "int32"), ("len3", [NL, 16], "int32"), ("lsn3", [NL, 16], "int32"),
        ("yo2", [W], "float32"), ("yo3", [W], "float32"), ("ly2", [W], "float32"), ("ly3", [W], "float32")):
    SCRATCH[_n] = ("sbuf", [128, H] + _s, _d)
SEMAPHORES = ["ldc", "lde", "lds", "out", "loc", "vec", "act", "pe", "gp", "ls2", "lsn2"] + [
    "%s%d" % (_a, _h) for _a in ("le2", "le3", "ls3", "len2", "len3", "lsn3", "ly2", "ly3") for _h in range(H)]


def rank_program(g, core, T, topo):
    rank = T.rank_of(core)
    if rank is None:
        return
    N = len(T.cores)
    nxt = T.cores[(rank + 3) % N]
    prv = T.cores[(rank + 7) % N]
    opp = T.cores[(rank + 4) % N]
    queue = {"v": g.vector, "s": g.scalar, "p": g.tensor, "g": g, "y": g.sync}
    engsem = {"v": "vec", "s": "act", "p": "pe", "g": "gp"}
    ops, lastw, rds, banks = [], {}, {}, {}

    def op(eng, cost, fn, r=(), w=(), bank=(), sem=None, val=0, lat=0.0):
        i = len(ops)
        dep = set()
        for k in r:
            if k in lastw: dep.add(lastw[k])
        for k in w:
            if k in lastw: dep.add(lastw[k])
            dep.update(rds.get(k, ()))
        for b in bank:
            dep.update(j for e, j in banks.setdefault(b, {}).items() if e != eng)
            banks[b][eng] = i
        dep.discard(i)
        for k in r: rds.setdefault(k, []).append(i)
        for k in w: lastw[k] = i; rds[k] = []
        ops.append(dict(eng=eng, cost=cost, fn=fn, dep=dep, sem=sem, val=val, lat=lat))
        return i

    def V(n, fn, r=(), w=(), bank=()):
        op("v", VO + n * CY, fn, r, w, bank)

    def S(n, fn, r=(), w=(), bank=()):
        op("s", SO + n * CY, fn, r, w, bank)

    def P(n, fn, r=(), w=(), bank=()):
        op("p", n * PCY, fn, r, w, bank)

    v, s, te = g.vector, g.scalar, g.tensor
    B = lambda n, h: T[n][:, h]
    ts, tt, scan, act, mm = v.tensor_scalar, v.tensor_tensor, v.tensor_tensor_scan, s.activation, te.matmul

    def dma(eng, q, out, in_, sem, w, lat):
        op(eng, 60.0, lambda: [(q.dma_start(out, in_), sem, 16)], (), w, sem=sem, val=16, lat=lat)

    dma("y", g.sync, T.en[:], T.enz[:], "lde", ["en"], 2000.0)
    dma("s", g.scalar, T.su[:], T.subs[:], "lds", ["su"], 2000.0)
    dma("y", g.sync, T.ct[:], T.cont[:], "ldc", ["ct"], 6000.0)

    V(128, lambda: v.memset(T.one[:], 1.0), w=["one"])
    op("g", 140, lambda: g.iota(T.pid[:], [[0, 1]], 0, 1), w=["pid"])
    V(1, lambda: ts(T.pbit[:], T.pid[:], 16, None, A.bitwise_and), ["pid"], ["pbit"])
    V(1, lambda: ts(T.modd[:], T.pbit[:], 1.0 / 16, None, A.mult), ["pbit"], ["modd"])
    V(1, lambda: ts(T.meven[:], T.pbit[:], -1.0 / 16, 1.0, A.mult, A.add), ["pbit"], ["meven"])
    op("g", 380, lambda: g.affine_select(T.idf[:], T.one[:], [[-1, 128]], A.is_equal, 0.0, 0, 1), ["one"], ["idf"])
    V(8, lambda: v.memset(T.g8a[:], 1.0), w=["g8a"])
    op("g", 190, lambda: g.affine_select(T.g8b[:], T.g8a[:], [[-16, 8]], A.is_ge, 0.0, 0, 1), ["g8a"], ["g8b"])
    op("g", 190, lambda: g.affine_select(T.g8c[:], T.g8b[:], [[16, 8]], A.is_ge, 0.0, 15, -1), ["g8b"], ["g8c"])

    def initial(k, src):
        xm, xt, nm = T["xm" + k], T["xt" + k], T["nm" + k]
        V(192, lambda: ts(xm[:, :, 0, :], T[src][:], T.meven[:], None, A.mult), [src, "meven"], ["xm0" + k])
        V(192, lambda: ts(xm[:, :, 1, :], T[src][:], T.modd[:], None, A.mult), [src, "modd"], ["xm1" + k])
        V(384, lambda: v.transpose(xt[:, :, :, :], xm[:, :, :, :]), ["xm0" + k, "xm1" + k], ["xt" + k])
        V(384, lambda: tt(nm[:], xt[:, :, 0, :], xt[:, :, 1, :], A.add), ["xt" + k], ["nm" + k])

    def lists(dst, src3, rk, wk):
        for c in range(NL):
            V(16, lambda c=c: v.tensor_copy(dst[:, c:W:NL], src3[:, c, :]), rk, [(wk, c)])

    initial("e", "en")
    for h in range(H):
        lists(T.m0l[:, h], T.nme[:, NL * h:NL * h + NL, :], ["nme"], ("m0l", h))
        if h == 0:
            initial("s", "su")
        lists(B("l0", h), T.nms[:, NL * h:NL * h + NL, :], ["nms"], ("l0", h))
        if h == 0:
            for n, val, d in IDENT:
                if d == "float16":
                    V(128, lambda n=n, val=val: ts(T[n][:], T.idf[:], val, None, A.mult), ["idf"], [n])
                else:
                    S(128, lambda n=n, val=val: act(T[n][:], T.idf[:], F.Copy, scale=val), ["idf"], [n])
            for n, val in (("selc", 0.5), ("seld", 65536.0)):
                V(80, lambda n=n: v.memset(T[n][:], 0.0), w=[n])
                V(8, lambda n=n, val=val: ts(T[n][:, 15:143:16], T.g8c[:], val, None, A.mult), ["g8c"], [n])
            V(W / 2, lambda: v.memset(T.kc8[:], 8.0), w=["kc8"])
            for n, pat, base in (("krow", [[4096, 16], [0, NL]], 0), ("kkeep", [[0, NL], [256, 16]], -2048), ("kfill", [[0, NL], [256, 16]], 2048)):
                op("g", 300, lambda n=n, pat=pat, base=base: g.iota(T[n][:], pat, base, 0, allow_small_or_imprecise_dtypes=True), w=[n])
            for n, val in (("x17", 0.0), ("a17", 0), ("pb", 0)):
                V(H * W17, lambda n=n, val=val: v.memset(T[n][:], val), w=[(n, q) for q in range(H)])
            for n in ("mx", "mn"):
                V(8, lambda n=n: v.memset(T[n][:, :, W17:W17 + 4], 0.0), w=[(n + "pad", q) for q in range(H)])
            for n, base, at, val, m in (("rk17", 0.0, (0,), BIG, 17), ("mk17", 1.0, (0,), 0.0, 17), ("rm17", 0.0, (15, 16), -1.0e6, 17),
                                        ("rn17", 0.0, (15, 16), 1.0e6, 17), ("tg17", 4096.0, (0,), -1.0e6, 17), ("kw", 2128.0, (15,), -1968.0, 17),
                                        ("mk16", 1.0, (0,), 0.0, 16), ("rm16", 0.0, (15,), -1.0e6, 16)):
                V(W17, lambda n=n, base=base: v.memset(T[n][:], base), w=[n])
                for a in at:
                    V(NL, lambda n=n, a=a, val=val, m=m: v.memset(T[n][:, a::m], val), w=[n])
    nloc = [0]

    def send(dst, land, out, in_, w, r):
        rid, pid = topo.addr(dst, core)
        m, ne = topo.mask(core, dst), len(topo.engines(core, dst))
        nloc[0] += ne
        i = op("g", 300, lambda: [(g.remote_dma(out, in_, T.sem[land], T.sem.loc, pid, rid, m), None, 0)], r)
        j = op("r", 0, None, (), w, sem=land, val=ne, lat=RLAT)
        ops[j]["dep"].add(i)

    send(opp, "ls2", T.ls2[:], T.m0l[:], ["ls2"], [(("m0l", h), c) for h in range(H) for c in range(NL)])
    send(opp, "lsn2", T.lsn2[:], T.nme[:], ["lsn2"], ["nme"])

    dn = [0]
    pw = T.pw
    for t in range(1, R + 1):
        for h in range(H):
            b = lambda n: B(n, h)
            K = lambda *n: [(x, h) for x in n]
            eb = "pe%d" % ((t * H + h) % 2)
            pE = T[eb]
            ck = T.pck[:, h % CKS, :, :, 0:NL]
            w0, w1 = pw[:, 2 * h, 0:W], pw[:, 2 * h + 1, 0:W]
            k0, k1 = [("pw", 2 * h)], [("pw", 2 * h + 1)]
            cs = slice(NL * h, NL * h + NL)
            if t == 1:
                el, ek = T.m0l[:, h], [(("m0l", h), c) for c in range(NL)]
                sl, sk = b("l0"), [(("l0", h), c) for c in range(NL)]
                en, enk, zn, znk = T.nme[:, cs, :], ["nme"], T.nms[:, cs, :], ["nms"]
            else:
                el, ek, en, enk = b("le%d" % t), K("le%d" % t), b("len%d" % t), K("len%d" % t)
                if t == 2:
                    sl, sk, zn, znk = T.ls2[:, h], ["ls2"], T.lsn2[:, cs, :], ["lsn2"]
                else:
                    sl, sk, zn, znk = b("ls3"), K("ls3"), b("lsn3"), K("lsn3")
            def gather(n, l, lk, a, z):
                for c in range(a, z, 64):
                    e = min(c + 64, z)
                    S(16 * (e - c) * 1.55, lambda c=c, e=e, y=b(n): act(y[:, 16 * (c - a):16 * (e - a)], T.ct[:].indirect(l[:, c:e]), F.Copy), ["ct"] + lk, [(n, h, c)])
                return [(n, h, c) for c in range(a, z, 64)]
            v15k = gather("v15", el, ek, W - NL, W)
            yk = gather("y", sl, sk, 0, W)
            for q in range(len(yk)): ops[-1 - q]["late"] = True
            vk = gather("v", el, ek, 0, W)

            def vdiff(q, p, x):
                a = PC * q
                mm(p[:, 0:PC], T.ip[:], x[:, a:a + PC], True, False)
                if q < NP - 1:
                    return mm(p[:, 0:PC], T.im[:], x[:, a + W:a + W + PC], False, True)
                mm(p[:, 0:PC - W], T.im[:], x[:, a + W:NV], False, False)
                return mm(p[:, PC - W:PC], T.im[:], x[:, 0:W], False, True)

            def ydiff(q, p, y, x):
                mm(p[:, 0:PC], T.ip[:], y[:, PC * q:PC * q + PC], True, False)
                for i in range(RP):
                    z = mm(p[:, W * i:W * i + W], T.im[:], x[:], False, i == RP - 1)
                return z

            def sums(p, sel, x, con):
                for m in range(16):
                    mm(p, sel[:, 15 - m:143 - m], x[:, m:NV:16], m == 0, False)
                return mm(p, T.ip[:], con[:], False, True)

            for kind in (1, 0):
                for q in range(NP):
                    pn = "pd%d" % (dn[0] % NDIFF); dn[0] += 1
                    a, z = PC * q, PC * q + PC
                    if kind == 0:
                        P(2 * PC, lambda q=q, p=T[pn], x=b("v"), f=vdiff: f(q, p, x), vk + ["ip", "im"], [pn], [pn])
                        S(PC, lambda a=a, z=z, p=T[pn], o=b("sg"): act(o[:, a:z], p[:, 0:PC], F.Sign, bias=-0.5), [pn], [("sg", h, q)], [pn])
                    else:
                        P(2 * PC, lambda q=q, p=T[pn], y=b("y"), x=b("v15"), f=ydiff: f(q, p, y, x), v15k + yk + ["ip", "im"], [pn], [pn])
                        S(PC, lambda a=a, z=z, p=T[pn], o=b("ab"): act(o[:, a:z], p[:, 0:PC], F.Abs), [pn], [("ab", h, q)], [pn])
            P(17 * W, lambda p=ck[:, 1], x=b("ab"), f=sums: f(p, T.seld, x, T.krow), [("ab", h, q) for q in range(NP)] + ["seld", "ip", "krow"], K("pk"), ["pck"])
            P(17 * W, lambda p=ck[:, 0], x=b("sg"), f=sums: f(p, T.selc, x, T.kc8), [("sg", h, q) for q in range(NP)] + ["selc", "ip", "kc8"], K("pc"), ["pck"])
            for c in range(NL):
                S(32, lambda c=c, p=ck, x=b("x17"): act(x[:, :, 17 * c:17 * c + 16], p[:, :, :, c], F.Copy), K("pc", "pk"), [("x17", h, c)], ["pck"])
            x17k = [("x17", h)] + [("x17", h, c) for c in range(NL)]
            V(W, lambda o=b("s2"), x=en: ts(o[:, 0, :, :], x[:], 7, None, A.arith_shift_right), enk, K("s2h"))
            V(W, lambda o=b("sl"), x=en: ts(o[:], x[:], 127, None, A.bitwise_and), enk, K("sl"))
            V(2 * W, lambda o=b("s2"), x=b("sl"): tt(o[:, 1, :, :], x[:], o[:, 0, :, :], A.add), K("sl", "s2h"), K("s2l"))
            V(W17, lambda x=b("x17"), o=b("cc"): scan(o[:], T.mk17[:], x[:, 0, :], 0.0, A.mult, A.add), x17k + ["mk17"], K("cc"))
            V(W17, lambda x=b("x17"), o=b("km"): scan(o[:], T.rk17[:], x[:, 1, :], 0.0, A.add, A.min), x17k + ["rk17"], K("km"))
            V(W17, lambda x=b("cc"), o=b("par"): ts(o[:], x[:], 1, None, A.bitwise_and), K("cc"), K("par"))
            V(NL, lambda x=b("km"), o=b("pb"): ts(o[:, 0::17], x[:, 15::17], 4096, None, A.bitwise_and), K("km"), K("pb"))
            V(W17, lambda x=b("par"), o=b("st"): ts(o[:], x[:], -8192.0, 4096.0, A.mult, A.add), K("par"), K("st"))
            V(W17, lambda x=b("pb"), o=b("od"): scan(o[:], T.tg17[:], x[:], 0.0, A.subtract, A.max), K("pb") + ["tg17"], K("od"))
            V(NL, lambda x=b("km"), o=b("st"): ts(o[:, 0::17], x[:, 15::17], 61440, None, A.bitwise_and), K("km"), K("st"))
            V(W17, lambda x=b("st"), o=b("pos"): scan(o[:], T.mk17[:], x[:], 0.0, A.mult, A.add), K("st") + ["mk17"], K("pos"))
            V(W17, lambda x=b("pos"), o=b("mx"): scan(o[:, W17 - 1::-1], T.rm17[:, ::-1], x[:, ::-1], 0.0, A.add, A.max), K("pos") + ["rm17"], K("mx"))
            V(W17, lambda x=b("pos"), o=b("mn"): scan(o[:, W17 - 1::-1], T.rn17[:, ::-1], x[:, ::-1], 0.0, A.add, A.min), K("pos") + ["rn17"], K("mn"))
            S(W17, lambda x=b("pos"), o=b("g1"): act(o[:], x[:], F.Sign, bias=63488.0, scale=-1.0), K("pos"), K("g1"))
            S(W17, lambda x=b("pos"), o=b("g2"): act(o[:], x[:], F.Sign, bias=-2048.0, scale=-1.0), K("pos"), K("g2"))
            S(W17, lambda x=b("x17"), o=b("w"): act(o[:], x[:, 0, :], F.Sign, bias=-9.5), x17k, K("w"))
            if t > 1:
                V(2 * W17, lambda x=b("x17"), o=b("d1"), a=b("a17"): tt(o[:], x[:, 0, :], a[:], A.subtract), x17k + K("a17"), K("d1"))
            dk, dx = (K("d1"), b("d1")) if t > 1 else (x17k, b("x17")[:, 0, :])
            S(W17, lambda x=dx, o=b("u"): act(o[:], x[:], F.Sign, bias=5.5, scale=-1.0), dk, K("u"))

            def usum(p, h):
                o = p[:, 0:NL, 32:49]
                mm(o, T.ip[:], T.kw[:], True, False)
                for n, c in (("od", "i4"), ("w", "i16"), ("u", "i32"), ("pos", "i16th"), ("g1", "i2048"), ("g2", "i2048")):
                    mm(o, T[c][:], B(n, h)[:], False, False)
                mm(o, T.im[:], B("mx", h)[:, 0:W17], False, False)
                mm(o, T.ip[:], B("mx", h)[:, 1:W17 + 1], False, False)
                mm(o, T.ip[:], B("mn", h)[:, 0:W17], False, False)
                return mm(o, T.im[:], B("mn", h)[:, 1:W17 + 1], False, True)
            P(11 * W17, lambda p=pE, h=h: usum(p, h), K("od", "pos", "g1", "g2", "u", "w", "mx", "mn", "mxpad", "mnpad") + ["ip", "im", "i16th", "i16", "i4", "i32", "i2048", "kw"], ["U" + eb], [eb])
            for a, sk2 in ((0, "s2h"), (1, "s2l")):
                V(W, lambda a=a, o=b("q1"), x=b("s2"), p=pE: tt(o[:, a, :, :], x[:, a, :, :], p[:, 0:NL, 32:48], A.add), K(sk2) + ["U" + eb], K("q1%d" % a), [eb])
            V(2 * W, lambda o=b("qx"), x=b("q1"): tt(o[:], x[:, :, :, 0::2], x[:, :, :, 1::2], A.max), K("q10", "q11"), K("qx"))
            V(2 * W, lambda o=b("qp"), x=b("q1"): tt(o[:, :, :, 0, :], x[:, :, :, 0::2], x[:, :, :, 1::2], A.min), K("q10", "q11"), K("qpe"))
            V(W, lambda o=b("qp"), x=b("qx"): ts(o[:, :, :, 1, :], x[:], -16640.0, None, A.add), K("qx"), K("qpo"))
            for p_ in range(8):
                V(W, lambda p_=p_, o=b("o1"), x=b("qp"): ts(o[:, :, :, p_, :, :], x[:], 512.0 * p_ - 2048.0, 512.0 * p_ - 1792.0, A.max, A.min), K("qpe", "qpo"), [("o1", h, p_)])

            def picked(p, q, o, n, f):
                for k in range(n):
                    for a, c in ((0, T.i127h), (1, T.iph)):
                        x = o[:, a, :, 8 * f:8 * f + 8, k] if n == 17 else o[:, a, :, 4 * f:4 * f + 4, :, k]
                        z = mm(p[:, 0:NL, q + 8 * f:q + 8 * f + 8], c[:], x, k == 0 and a == 0, k == n - 1 and a == 1)
                return z
            for f in range(2):
                P(16 * max(64, W // 2), lambda p=pE, o=b("o1"), f=f, pk=picked: pk(p, 0, o, 8, f), [("o1", h, p_) for p_ in range(4 * f, 4 * f + 4)] + ["iph", "i127h"], ["E%d" % f + eb], [eb])
            V(W, lambda o=b("ei"), p=pE: v.tensor_copy(o[:], p[:, 0:NL, 0:16]), ["E0" + eb, "E1" + eb], K("ei"), [eb])
            V(W, lambda o=b("xx"), x=b("ei"): ts(o[:], x[:], 16383, None, A.bitwise_and), K("ei"), K("xx"))
            V(W, lambda x=b("xx"), o=b("dl"): ts(o[:], x[:], 12288.0, None, A.is_ge), K("xx"), K("dl"))
            V(W, lambda x=b("dl"), o=b("ii"): scan(o[:], T.mk16[:], x[:], 0.0, A.mult, A.add), K("dl") + ["mk16"], K("ii"))
            V(W, lambda x=b("ii"), o=b("nb"): scan(o[:, ::-1], T.rm16[:, ::-1], x[:, ::-1], 0.0, A.add, A.max), K("ii") + ["rm16"], K("nb"))

            def tsum(p, h):
                o = p[:, 0:NL, 32:48]
                mm(o, T.ip[:], T.kkeep[:], True, False)
                mm(o, T.i8192[:], B("dl", h)[:], False, False)
                mm(o, T.im256[:], B("ii", h)[:], False, True)
                o = p[:, 0:NL, 0:16]
                mm(o, T.ip[:], T.kfill[:], True, False)
                return mm(o, T.im256[:], B("nb", h)[:], False, True)
            P(5 * W, lambda p=pE, h=h: tsum(p, h), K("dl", "ii", "nb") + ["i8192", "im256", "ip", "kkeep", "kfill"], ["T" + eb, "U" + eb, "E0" + eb, "E1" + eb], [eb])
            V(W, lambda x=b("xx"), o=w0: ts(o, x[:], -8192.0, 0.0, A.add, A.max), K("xx"), k0)
            V(W, lambda x=b("xx"), o=b("n32"): ts(o[:], x[:], 4096.0, 32.0, A.is_lt, A.mult), K("xx"), K("n32"))
            V(W, lambda x=b("xx"), o=w1, t=t: ts(o, x[:], 8192.0, 77.0 * t, A.is_ge, A.mult), K("xx"), k1)
            V(W, lambda x=b("n32"), o=w0: tt(o, x[:], o, A.add), K("n32"), k0)
            V(W, lambda x=b("xx"), o=w1: tt(o, x[:], o, A.add), K("xx"), k1)
            V(W, lambda x=zn, o=b("az"), y=w0: tt(o[:], x, y, A.mult), znk + k0, K("az"))
            V(W, lambda x=b("az"), o=b("sf"): ts(o[:], x[:], 5, 4095, A.arith_shift_right, A.bitwise_and), K("az"), K("sf"))
            V(W, lambda x=b("sf"), o=b("b2"), y=w1: tt(o[:], x[:], y, A.add), K("sf") + k1, K("b2"))
            V(W, lambda x=b("b2"), o=b("n2"): ts(o[:, 0, :], x[:], 7, 31, A.arith_shift_right, A.bitwise_and), K("b2"), K("n2h"))
            V(W, lambda x=b("b2"), o=b("n2"): ts(o[:, 1, :], x[:], 127, None, A.bitwise_and), K("b2"), K("n2l"))
            for a, sk2 in ((0, "s2h"), (1, "s2l")):
                V(W, lambda a=a, o=b("q2"), x=b("s2"), p=pE: tt(o[:, a, :, 16:32], x[:, a, :, :], p[:, 0:NL, 0:16], A.add), K(sk2) + ["T" + eb], K("q2b%d" % a), [eb])
            V(W, lambda x=b("n2"), p=pE, o=w0: tt(o, x[:, 0, :], p[:, 0:NL, 32:48], A.add), K("n2h") + ["T" + eb], k0, [eb])
            V(W, lambda x=b("n2"), o=b("q2"), y=w0: tt(o[:, 1, :, 0:16], x[:, 1, :], y, A.add), K("n2l") + k0, K("q2a1"))
            V(W, lambda o=b("q2"), y=w0: v.tensor_copy(o[:, 0, :, 0:16], y), k0, K("q2a0"))
            for i in range(16):
                V(W17, lambda i=i, o=b("o2"), x=b("q2"): ts(o[:, :, :, i, :], x[:, :, :, i:i + 17], 256.0 * i - 2048.0, 256.0 * i - 1792.0, A.max, A.min), K("q2a0", "q2a1", "q2b0", "q2b1"), [("o2", h, i)])
            for f in range(2):
                P(34 * max(64, W // 2), lambda p=pE, o=b("o2"), f=f, pk=picked: pk(p, 16, o, 17, f), [("o2", h, i) for i in range(8 * f, 8 * f + 8)] + ["iph", "i127h"], ["R%d" % f + eb], [eb])
            nm, nmk = b("nm%d" % t), K("nm%d" % t)
            V(W, lambda o=b("fi"), p=pE: v.tensor_copy(o[:], p[:, 0:NL, 16:32]), ["R0" + eb, "R1" + eb], K("fi"), [eb])
            V(W, lambda o=nm, x=b("fi"): ts(o[:], x[:], 4095, None, A.bitwise_and), K("fi"), nmk)
            if t < R:
                n = t + 1
                lists(b("ml%d" % t), nm, nmk, ("ml%d" % t, h))
                mk = [(("ml%d" % t, h), c) for c in range(NL)]
                send(nxt, "le%d%d" % (n, h), b("le%d" % n)[:], b("ml%d" % t)[:], K("le%d" % n), mk)
                send(nxt, "len%d%d" % (n, h), b("len%d" % n)[:], nm[:], K("len%d" % n), nmk)
                if t + 2 <= R:
                    send(prv, "ls3%d" % h, b("ls3")[:], b("ml%d" % t)[:], K("ls3"), mk)
                    send(prv, "lsn3%d" % h, b("lsn3")[:], nm[:], K("lsn3"), nmk)
                V(W, lambda x=b("nb"), o=b("ni"): v.tensor_copy(o[:], x[:]), K("nb"), K("ni"))
                V(W, lambda x=b("ni"), o=b("a17"): ts(o[:, :, 0:16], x[:], 1, None, A.bitwise_and), K("ni"), K("a17"))
            if t >= R - 1:
                V(W, lambda x=nm, o=b("tm"): ts(o[:, :, 0, :], x[:], T.meven[:], None, A.mult), nmk + ["meven"], K("tm0"))
                V(W, lambda x=nm, o=b("tm"): ts(o[:, :, 1, :], x[:], T.modd[:], None, A.mult), nmk + ["modd"], K("tm1"))
                V(2 * W, lambda x=b("tm"), o=b("tt"): v.transpose(o[:], x[:]), K("tm0", "tm1"), K("tt"))
                V(2 * W, lambda x=b("tt"), o=b("yo%d" % t): tt(o[:], x[:, :, 0, :], x[:, :, 1, :], A.add), K("tt"), K("yo%d" % t))
                send(nxt if t == R else prv, "ly%d%d" % (t, h), b("ly%d" % t)[:], b("yo%d" % t)[:], K("ly%d" % t), K("yo%d" % t))
                y = T.yenz if t == R else T.ysub
                op("y", 60, lambda y=y, x=b("ly%d" % t), h=h: [(g.sync.dma_start(y[:, W * h:W * h + W], x[:]), "out", 16)], K("ly%d" % t))

    n = len(ops)
    succ = [[] for i in range(n)]
    for i, o in enumerate(ops):
        for d in o["dep"]: succ[d].append(i)
        o["pr"] = i + (LATE if o.get("late") else 0)
    by_pr = sorted(range(n), key=lambda i: ops[i]["pr"])

    def schedule(known):
        left = [len(o["dep"]) for o in ops]
        ready = [0.0] * n
        free, order, cand, urgent, out = {}, [], {}, {}, set()
        if known:
            for i in by_pr: urgent.setdefault(ops[i]["eng"], []).append(i)
        end = 0.0
        for i in range(n):
            if not left[i]: cand.setdefault(ops[i]["eng"], []).append(i)
        while True:
            best = None
            for e, c in cand.items():
                if not c: continue
                f = free.get(e, 0.0) if e != "r" else 0.0
                starts = []
                for i in c:
                    st = max(ready[i], f)
                    if known and ops[i]["cost"] > HOLD:
                        lim = st + AHEAD * ops[i]["cost"]
                        for j in urgent[e]:
                            if ops[j]["pr"] >= ops[i]["pr"]: break
                            if j not in out and left[j] and st < known[j] < lim: st = known[j] + 1.0
                    starts.append((st, i))
                lo = min(starts)[0]
                pr, st, i = min((ops[i]["pr"], st, i) for st, i in starts if st <= lo + 20.0)
                if best is None or (st, i) < best[0]: best = ((st, i), e, i)
            if best is None: break
            (st, _), e, i = best
            cand[e].remove(i)
            out.add(i)
            free[e] = st + ops[i]["cost"]
            fin = free[e] + ops[i]["lat"]
            end = max(end, fin)
            order.append(i)
            for j in succ[i]:
                ready[j] = max(ready[j], fin + WAKE)
                left[j] -= 1
                if not left[j]: cand.setdefault(ops[j]["eng"], []).append(j)
        return end, order, ready

    best, known = None, None
    for k in range(PASSES):
        end, order, known = schedule(known)
        if best is None or end < best[0]: best = (end, order)

    count, done, waited, ndma = {}, {}, {}, 0
    for i in best[1]:
        o = ops[i]
        e = o["eng"]
        if e == "r":
            done[i] = (o["sem"], o["val"])
            continue
        need = {}
        for d in o["dep"]:
            sm, val = done[d]
            need[sm] = max(need.get(sm, 0), val)
        for sm in sorted(need):
            if waited.get((e, sm), 0) < need[sm]:
                queue[e].wait_ge(T.sem[sm], need[sm])
                waited[(e, sm)] = need[sm]
        x = o["fn"]()
        if isinstance(x, list):
            ins, sm, inc = x[0]
            if sm is not None:
                ins.then_inc(T.sem[sm], inc)
                if sm == "out": ndma += inc
            done[i] = (sm, o["val"]) if sm else ("loc", 0)
        else:
            sm = engsem[e]
            x.then_inc(T.sem[sm], 1)
            count[sm] = count.get(sm, 0) + 1
            done[i] = (sm, count[sm])
    g.sync.wait_ge(T.sem.out, ndma)
    g.wait_ge(T.sem.loc, nloc[0])
    for sm in count:
        g.wait_ge(T.sem[sm], count[sm])
